import numpy as np
import ml_dtypes


def mxq(x, axis, fmt="e4m3"):
    dtype, down = {"e4m3": (ml_dtypes.float8_e4m3fn, 7), "e5m2": (ml_dtypes.float8_e5m2, 14)}[fmt]
    v = np.moveaxis(np.asarray(x, np.float32).astype(ml_dtypes.bfloat16).astype(np.float64), axis, -1)
    blocks = v.reshape(v.shape[:-1] + (-1, 32))
    amax = np.abs(blocks).max(-1, keepdims=True)
    byte = np.maximum(np.where(amax > 0, np.frexp(amax)[1] - 1 + 127, 0) - down, 1)
    scale = np.exp2(byte - 127.0)
    codes = (blocks / scale).astype(np.float32).astype(dtype).astype(np.float64)
    return np.moveaxis((codes * scale).reshape(v.shape), -1, axis)


WIDE = False


def mx_kscale(k):
    if not WIDE:
        return np.ones(k)
    levels = np.array([10, -10, 5, -5, 0])
    if k % 512:
        return np.exp2(np.random.permutation(np.resize(levels, k // 32))).repeat(32)
    a = np.empty((k // 512, 16))
    for p in range(k // 512):
        a[p, :8] = np.random.permutation(np.resize(levels, 8))
        for g in range(8):
            far = levels[np.abs(levels - a[p, g]) >= 10]
            a[p, g + 8] = far[np.random.randint(len(far))]
    return np.exp2(a.ravel()).repeat(32)


def f64(x):
    return np.asarray(x).astype(np.float64)


def striped(idx):
    return np.tile(idx.reshape(-1, 16).T, (8, 1)).astype(np.uint16)


def unstriped(offs):
    return offs[:16].T.reshape(-1).astype(np.int64)


def pack_weight(w):
    k, n = w.shape
    w = f64(np.asarray(w, np.float32).astype(ml_dtypes.bfloat16)).reshape(k // 32, 32, n)
    amax = np.abs(w).max(1)
    byte = np.clip(np.where(amax > 0, np.frexp(amax)[1] - 1 + 127 - 7, 1), 1, 254)
    scaled = (w * np.exp2(127.0 - byte)[:, None, :]).reshape(k, n).astype(np.float32)
    words = np.ascontiguousarray(scaled.reshape(k // 512, 128, 4, n).transpose(0, 1, 3, 2)).astype(ml_dtypes.float8_e4m3fn).view(np.uint8)
    return words, np.ascontiguousarray(byte.astype(np.uint8).reshape(k // 512, 16, n))


def unpack_weight(words, scales):
    g, p, n, _ = words.shape
    vals = np.ascontiguousarray(words).view(ml_dtypes.float8_e4m3fn).astype(np.float64) * np.repeat(np.exp2(scales.astype(np.float64) - 127.0), 8, axis=1)[..., None]
    return vals.transpose(0, 1, 3, 2).reshape(g * 512, n)


def silu(v):
    return v / (1.0 + np.exp(-np.maximum(v, -700.0)))


K, T, S, H, N = 1024, 2048, 512, 512, 128
P = 2 ** 7


def setup_inputs():
    n = np.random.standard_normal
    s = mx_kscale(K)[:, None]
    u = mx_kscale(H)
    packed_xT = pack_weight(n((K, T)) * s)
    return {
        "x_words": packed_xT[0],
        "x_scales": packed_xT[1],
        "gate": np.tile(np.random.uniform(0.2, 1.0, T), (P, 1)).astype(np.float32),
        "w1": (n((K, H)) / np.sqrt(K) / s * u).astype(np.float32),
        "w2": (n((H, N)) / np.sqrt(H) / u[:, None]).astype(np.float32),
        "offs": striped(np.random.permutation(T)[:S]),
    }


def reference(x_words, x_scales, gate, w1, w2, offs):
    xq = unpack_weight(x_words, x_scales)[:, unstriped(offs)]
    h = silu(mxq(f64(w1), 0, "e4m3").T @ xq)
    y = mxq(f64(w2), 0, "e4m3").T @ mxq(h, 0, "e4m3")
    g = f64(gate)[:1][:, unstriped(offs)]
    out = np.zeros((N, T))
    out[:, unstriped(offs)] = y * g
    return out

@@ -1,0 +1,176 @@
+from contextlib import ExitStack
+
+import concourse.mybir as mybir
+from concourse.masks import make_identity
+
+K, T, S, H, N = 1024, 2048, 512, 512, 128
+FLOPS = 2 * S * (K * H + H * N)
+BYTES = K * T + (K // 32) * T + 4 * T + 4 * K * H + 4 * H * N + 2 * 128 * (S // 16) + 4 * N * T
+
+F32 = mybir.dt.float32
+BF16 = mybir.dt.bfloat16
+I32 = mybir.dt.int32
+U32 = mybir.dt.uint32
+U16 = mybir.dt.uint16
+U8 = mybir.dt.uint8
+FP8X4 = mybir.dt.float8_e4m3fn_x4
+SILU = mybir.ActivationFunctionType.Silu
+MULT = mybir.AluOpType.mult
+
+P = 128
+PACK = 4
+PASSES = K // (P * PACK)
+CH = 128
+HALF = 256
+
+
+def tile_picked_modgate_mlpsilu_p_kernel(tc, x_words, x_scales, gate, w1, w2, offs, out):
+    nc = tc.nc
+    with ExitStack() as ctx:
+        keep = ctx.enter_context(tc.tile_pool(name="keep", bufs=1))
+        psum = ctx.enter_context(tc.psum_pool(name="psum", bufs=1))
+
+        offsets = keep.tile([P, S // 16], U16, name="offsets")
+        xs_win = keep.tile([P, T], U8, name="xs_win", align_bytes=64)
+        nc.gpsimd.memset(xs_win[:].bitcast(I32), 0)
+
+        w1_raw = [keep.tile([P, PACK, H], F32, name="w1_raw0")]
+        g16 = keep.tile([P, T // P], F32, name="g16")
+
+        nc.sync.dma_start(offsets[:], offs)
+        nc.sync.dma_start(out=w1_raw[0][:], in_=w1[0:512, :].rearrange("(p j) c -> p j c", j=PACK))
+        nc.scalar.dma_start(out=g16[:], in_=gate[0:1, :].rearrange("o (p c) -> p (o c)", p=P))
+        for q in range(4):
+            nc.scalar.dma_start(
+                out=xs_win[32 * q : 32 * q + 8, :].bitcast(I32),
+                in_=x_scales[:, 4 * q : 4 * q + 4, :].bitcast(I32),
+            )
+        warm_in = keep.tile([P, 8], F32, name="warm_in", tag="x_win0", align_bytes=64)
+        warm_out = keep.tile([P, 8], F32, name="warm_out", tag="x_win1", align_bytes=64)
+        warm_bias = keep.tile([P, 1], F32, name="warm_bias", tag="w1_raw1")
+        nc.vector.memset(warm_in[:], 0.0)
+        nc.vector.memset(warm_bias[:], 0.0)
+        nc.scalar.activation(out=warm_out[:], in_=warm_in[:], func=SILU, bias=warm_bias[:])
+        w1_raw.append(keep.tile([P, PACK, H], F32, name="w1_raw1"))
+        nc.sync.dma_start(out=w1_raw[1][:], in_=w1[512:1024, :].rearrange("(p j) c -> p j c", j=PACK))
+        x_win = [keep.tile([P, T], I32, name="x_win%d" % z, align_bytes=64) for z in range(PASSES)]
+        for z in range(PASSES):
+            nc.sync.dma_start(out=x_win[z][:], in_=x_words[z].rearrange("p n t -> p (n t)").bitcast(I32))
+
+        ident = keep.tile([P, P], F32, name="ident")
+        make_identity(nc, ident[:])
+        out_win = keep.tile([P, T], F32, name="out_win")
+        nc.vector.memset(out_win[:], 0.0)
+
+        g_win = keep.tile([P, T], F32, name="g_win", align_bytes=64)
+        for b in range(4):
+            gb = psum.tile([P, 4, P], F32, name="gb%d" % b, tag="acc%d" % b)
+            for c in range(4):
+                col = 4 * b + c
+                nc.tensor.transpose(gb[:, c, :], g16[:, col : col + 1].to_broadcast([P, P]), ident[:])
+            nc.scalar.copy(
+                out=g_win[:].rearrange("p (n c) -> p n c", c=T // P)[:, :, 4 * b : 4 * b + 4],
+                in_=gb[:].rearrange("p c n -> p n c"),
+            )
+
+        xs = keep.tile([P, S], U8, name="xs", align_bytes=64)
+        nc.vector.tensor_copy(xs[:], xs_win[:].indirect(offsets[:]))
+
+        w1_codes = []
+        w1_scales = []
+        for z in range(PASSES):
+            grouped = keep.tile([P, PACK, P, PACK], BF16, name="w1_bf%d" % z, align_bytes=64)
+            src = w1_raw[z][:].rearrange("p j (b t r) -> p t b r j", t=PACK, r=8)
+            dst = grouped[:].rearrange("p t (b r) j -> p t b r j", r=8)
+            share = (3, 2)[z]
+            nc.vector.tensor_copy(out=dst[:, 0:share], in_=src[:, 0:share])
+            nc.scalar.copy(out=dst[:, share:4], in_=src[:, share:4])
+            codes = keep.tile([P, H], U32, name="w1_codes%d" % z, tag=("w1_codes0", "xs_win")[z], align_bytes=64)
+            scales = keep.tile([P, H], U8, name="w1_scales%d" % z, tag=("w1_scales0", "g_win")[z], align_bytes=64)
+            nc.vector.quantize_mx(out=codes[:].bitcast(FP8X4), scales=scales[:], in_=grouped[:].rearrange("p t m j -> p (t m j)"))
+            w1_codes.append(codes)
+            w1_scales.append(scales)
+            if z == 0:
+                g = keep.tile([P, S], F32, name="g")
+                nc.vector.tensor_copy(g[:], g_win[:].indirect(offsets[:]))
+
+        w2_raw = keep.tile([P, PACK, N], F32, name="w2_raw", tag="w1_raw0")
+        w2_rows = w2.rearrange("(b t r) n -> t b r n", t=PACK, r=8)
+        for t in range(PACK):
+            nc.sync.dma_start(out=w2_raw[:, t, :], in_=w2_rows[t])
+
+        xg = []
+        for z in range(PASSES):
+            picked = keep.tile([P, S], U32, name="xg%d" % z, tag=("w1_bf1", "x_win0")[z], align_bytes=64)
+            for u in range(2):
+                nc.vector.tensor_copy(
+                    picked[:, u * HALF : (u + 1) * HALF],
+                    x_win[z][:].bitcast(U32).indirect(offsets[:, 16 * u : 16 * u + 16]),
+                )
+            xg.append(picked)
+
+        def first_layer(acc, c, t, z):
+            m = slice(t * P, (t + 1) * P)
+            nc.tensor.matmul_mx(
+                out=acc[:, t, :],
+                lhsT=w1_codes[z][:, m].bitcast(FP8X4),
+                lhsT_scale=w1_scales[z][:, m],
+                rhs=xg[z][:, c * CH : (c + 1) * CH].bitcast(FP8X4),
+                rhs_scale=xs[4 * z : P, c * CH : (c + 1) * CH],
+                start=(z == 0),
+                stop=(z == PASSES - 1),
+            )
+
+        warm_ps = psum.tile([P, 2, HALF], F32, name="warm_ps")
+        for i in range(4):
+            nc.tensor.matmul_mx(
+                out=warm_ps[:, i % 2, :],
+                lhsT=w1_codes[0][:, 0:P].bitcast(FP8X4),
+                lhsT_scale=w1_scales[0][:, 0:P],
+                rhs=xg[0][:, 0:HALF].bitcast(FP8X4),
+                rhs_scale=xs[:, 0:HALF],
+                start=True,
+                stop=True,
+            )
+        accs = [psum.tile([P, PACK, CH], F32, name="acc%d" % c) for c in range(S // CH)]
+        for c in range(S // CH):
+            first_layer(accs[c], c, 0, 0)
+
+        w2_bf = keep.tile([P, N, PACK], BF16, name="w2_bf", tag="x_win1", align_bytes=64)
+        nc.vector.tensor_copy(
+            out=w2_bf[:].rearrange("p (c i) j -> p c j i", i=4), in_=w2_raw[:].rearrange("p j (c i) -> p c j i", i=4)
+        )
+        w2_codes = keep.tile([P, N], U32, name="w2_codes", align_bytes=64)
+        w2_scales = keep.tile([P, N], U8, name="w2_scales", align_bytes=64)
+        nc.vector.quantize_mx(out=w2_codes[:].bitcast(FP8X4), scales=w2_scales[:], in_=w2_bf[:].rearrange("p n j -> p (n j)"))
+
+        y_ps = [psum.tile([P, HALF], F32, name="y_ps%d" % u) for u in range(2)]
+        y_sb = [keep.tile([P, HALF], F32, name="y_sb%d" % u) for u in range(2)]
+        for c in range(S // CH):
+            u, v = divmod(c, 2)
+            sub = slice(v * CH, (v + 1) * CH)
+            acc = accs[c]
+            for t in range(PACK):
+                for z in range(PASSES):
+                    if (t, z) != (0, 0):
+                        first_layer(acc, c, t, z)
+            h_bf = keep.tile([P, CH, PACK], BF16, name="h_bf%d" % c, align_bytes=64)
+            nc.scalar.activation(out=h_bf[:], in_=acc[:].rearrange("p t n -> p n t"), func=SILU)
+            h_codes = keep.tile([P, CH], U32, name="h_codes%d" % c, align_bytes=64)
+            h_scales = keep.tile([P, CH], U8, name="h_scales%d" % c, align_bytes=64)
+            nc.vector.quantize_mx(out=h_codes[:].bitcast(FP8X4), scales=h_scales[:], in_=h_bf[:].rearrange("p n t -> p (n t)"))
+            nc.tensor.matmul_mx(
+                out=y_ps[u][:, sub],
+                lhsT=w2_codes[:].bitcast(FP8X4),
+                lhsT_scale=w2_scales[:],
+                rhs=h_codes[:].bitcast(FP8X4),
+                rhs_scale=h_scales[:],
+                start=True,
+                stop=True,
+            )
+        for u in range(2):
+            nc.scalar.copy(out=y_sb[u][:], in_=y_ps[u][:])
+            nc.vector.tensor_tensor(
+                out_win[:].indirect(offsets[:, 16 * u : 16 * u + 16]), y_sb[u][:], g[:, u * HALF : (u + 1) * HALF], MULT
+            )
+        nc.sync.dma_start(out=out, in_=out_win[:])

@@ -28,29 +28,31 @@ def tile_picked_modgate_mlpsilu_p_kernel(tc, x_words, x_scales, gate, w1, w2, of
     nc = tc.nc
     with ExitStack() as ctx:
         keep = ctx.enter_context(tc.tile_pool(name="keep", bufs=1))
+        shared = ctx.enter_context(tc.tile_pool(name="shared", bufs=1))
         psum = ctx.enter_context(tc.psum_pool(name="psum", bufs=1))
 
         offsets = keep.tile([P, S // 16], U16, name="offsets")
+        g16 = keep.tile([P, T // P], F32, name="g16")
+        w1_raw = [keep.tile([P, PACK, H], F32, name="w1_raw0")]
+        nc.sync.dma_start(out=g16[:], in_=gate[0:1, :].rearrange("o (p c) -> p (o c)", p=P))
+        nc.sync.dma_start(out=w1_raw[0][:], in_=w1[0:512, :].rearrange("(p j) c -> p j c", j=PACK))
+        nc.sync.dma_start(offsets[:], offs)
+
         xs_win = keep.tile([P, T], U8, name="xs_win", align_bytes=64)
         nc.gpsimd.memset(xs_win[:].bitcast(I32), 0)
-
-        w1_raw = [keep.tile([P, PACK, H], F32, name="w1_raw0")]
-        g16 = keep.tile([P, T // P], F32, name="g16")
-
-        nc.sync.dma_start(offsets[:], offs)
-        nc.sync.dma_start(out=w1_raw[0][:], in_=w1[0:512, :].rearrange("(p j) c -> p j c", j=PACK))
-        nc.scalar.dma_start(out=g16[:], in_=gate[0:1, :].rearrange("o (p c) -> p (o c)", p=P))
         for q in range(4):
-            nc.scalar.dma_start(
+            nc.sync.dma_start(
                 out=xs_win[32 * q : 32 * q + 8, :].bitcast(I32),
                 in_=x_scales[:, 4 * q : 4 * q + 4, :].bitcast(I32),
             )
+
         warm_in = keep.tile([P, 8], F32, name="warm_in", tag="x_win0", align_bytes=64)
         warm_out = keep.tile([P, 8], F32, name="warm_out", tag="x_win1", align_bytes=64)
         warm_bias = keep.tile([P, 1], F32, name="warm_bias", tag="w1_raw1")
         nc.vector.memset(warm_in[:], 0.0)
         nc.vector.memset(warm_bias[:], 0.0)
         nc.scalar.activation(out=warm_out[:], in_=warm_in[:], func=SILU, bias=warm_bias[:])
+
         w1_raw.append(keep.tile([P, PACK, H], F32, name="w1_raw1"))
         nc.sync.dma_start(out=w1_raw[1][:], in_=w1[512:1024, :].rearrange("(p j) c -> p j c", j=PACK))
         x_win = [keep.tile([P, T], I32, name="x_win%d" % z, align_bytes=64) for z in range(PASSES)]
@@ -68,54 +70,61 @@ def tile_picked_modgate_mlpsilu_p_kernel(tc, x_words, x_scales, gate, w1, w2, of
             for c in range(4):
                 col = 4 * b + c
                 nc.tensor.transpose(gb[:, c, :], g16[:, col : col + 1].to_broadcast([P, P]), ident[:])
-            nc.scalar.copy(
+            nc.vector.tensor_copy(
                 out=g_win[:].rearrange("p (n c) -> p n c", c=T // P)[:, :, 4 * b : 4 * b + 4],
                 in_=gb[:].rearrange("p c n -> p n c"),
             )
 
-        xs = keep.tile([P, S], U8, name="xs", align_bytes=64)
+        g = keep.tile([P, S], F32, name="g")
+        nc.vector.tensor_copy(g[:], g_win[:].indirect(offsets[:]))
+
+        xs = keep.tile([P, S], U8, name="xs", tag="g_win", align_bytes=64)
         nc.vector.tensor_copy(xs[:], xs_win[:].indirect(offsets[:]))
 
+        w1_bf = []
         w1_codes = []
         w1_scales = []
         for z in range(PASSES):
-            grouped = keep.tile([P, PACK, P, PACK], BF16, name="w1_bf%d" % z, align_bytes=64)
-            src = w1_raw[z][:].rearrange("p j (b t r) -> p t b r j", t=PACK, r=8)
-            dst = grouped[:].rearrange("p t (b r) j -> p t b r j", r=8)
-            share = (3, 2)[z]
-            nc.vector.tensor_copy(out=dst[:, 0:share], in_=src[:, 0:share])
-            nc.scalar.copy(out=dst[:, share:4], in_=src[:, share:4])
-            codes = keep.tile([P, H], U32, name="w1_codes%d" % z, tag=("w1_codes0", "xs_win")[z], align_bytes=64)
-            scales = keep.tile([P, H], U8, name="w1_scales%d" % z, tag=("w1_scales0", "g_win")[z], align_bytes=64)
-            nc.vector.quantize_mx(out=codes[:].bitcast(FP8X4), scales=scales[:], in_=grouped[:].rearrange("p t m j -> p (t m j)"))
-            w1_codes.append(codes)
-            w1_scales.append(scales)
             if z == 0:
-                g = keep.tile([P, S], F32, name="g")
-                nc.vector.tensor_copy(g[:], g_win[:].indirect(offsets[:]))
+                grouped = keep.tile([P, PACK, P, PACK], BF16, name="w1_bf0", align_bytes=64)
+            else:
+                grouped = shared.tile([P, PACK, P, PACK], BF16, name="w1_bf1", align_bytes=64, offset=0)
+            src = w1_raw[z][:].rearrange("p j (b t c i) -> p t b c j i", t=PACK, c=2, i=4)
+            dst = grouped[:].rearrange("p t (b c i) j -> p t b c j i", c=2, i=4)
+            for t in range(PACK):
+                nc.scalar.copy(out=dst[:, t], in_=src[:, t])
+            w1_bf.append(grouped)
 
         w2_raw = keep.tile([P, PACK, N], F32, name="w2_raw", tag="w1_raw0")
         w2_rows = w2.rearrange("(b t r) n -> t b r n", t=PACK, r=8)
         for t in range(PACK):
             nc.sync.dma_start(out=w2_raw[:, t, :], in_=w2_rows[t])
 
-        xg = []
-        for z in range(PASSES):
-            picked = keep.tile([P, S], U32, name="xg%d" % z, tag=("w1_bf1", "x_win0")[z], align_bytes=64)
-            for u in range(2):
-                nc.vector.tensor_copy(
-                    picked[:, u * HALF : (u + 1) * HALF],
-                    x_win[z][:].bitcast(U32).indirect(offsets[:, 16 * u : 16 * u + 16]),
-                )
-            xg.append(picked)
+        def quantise_w1(z, tag):
+            codes = keep.tile([P, H], U32, name="w1_codes%d" % z, tag=tag, align_bytes=64)
+            scales = keep.tile([P, H], U8, name="w1_scales%d" % z, align_bytes=64)
+            nc.vector.quantize_mx(out=codes[:].bitcast(FP8X4), scales=scales[:], in_=w1_bf[z][:].rearrange("p t m j -> p (t m j)"))
+            w1_codes.append(codes)
+            w1_scales.append(scales)
+
+        quantise_w1(0, "xs_win")
+        xg0 = keep.tile([P, S], U32, name="xg0", tag="w1_bf0", align_bytes=64)
+        nc.vector.tensor_copy(xg0[:], x_win[0][:].bitcast(U32).indirect(offsets[:]))
+        quantise_w1(1, "x_win0")
+        xg1 = []
+        for u in range(2):
+            picked = shared.tile([P, HALF], U32, name="xg1%d" % u, align_bytes=64, offset=4 * HALF * u)
+            nc.vector.tensor_copy(picked[:], x_win[1][:].bitcast(U32).indirect(offsets[:, 16 * u : 16 * u + 16]))
+            xg1.append(picked)
 
         def first_layer(acc, c, t, z):
             m = slice(t * P, (t + 1) * P)
+            words = xg0[:, c * CH : (c + 1) * CH] if z == 0 else xg1[c // 2][:, (c % 2) * CH : (c % 2 + 1) * CH]
             nc.tensor.matmul_mx(
                 out=acc[:, t, :],
                 lhsT=w1_codes[z][:, m].bitcast(FP8X4),
                 lhsT_scale=w1_scales[z][:, m],
-                rhs=xg[z][:, c * CH : (c + 1) * CH].bitcast(FP8X4),
+                rhs=words.bitcast(FP8X4),
                 rhs_scale=xs[4 * z : P, c * CH : (c + 1) * CH],
                 start=(z == 0),
                 stop=(z == PASSES - 1),
@@ -127,7 +136,7 @@ def tile_picked_modgate_mlpsilu_p_kernel(tc, x_words, x_scales, gate, w1, w2, of
                 out=warm_ps[:, i % 2, :],
                 lhsT=w1_codes[0][:, 0:P].bitcast(FP8X4),
                 lhsT_scale=w1_scales[0][:, 0:P],
-                rhs=xg[0][:, 0:HALF].bitcast(FP8X4),
+                rhs=xg0[:, 0:HALF].bitcast(FP8X4),
                 rhs_scale=xs[:, 0:HALF],
                 start=True,
                 stop=True,

@@ -32,11 +32,13 @@ def tile_picked_modgate_mlpsilu_p_kernel(tc, x_words, x_scales, gate, w1, w2, of
         psum = ctx.enter_context(tc.psum_pool(name="psum", bufs=1))
 
         offsets = keep.tile([P, S // 16], U16, name="offsets")
-        g16 = keep.tile([P, T // P], F32, name="g16")
         w1_raw = [keep.tile([P, PACK, H], F32, name="w1_raw0")]
-        nc.sync.dma_start(out=g16[:], in_=gate[0:1, :].rearrange("o (p c) -> p (o c)", p=P))
-        nc.sync.dma_start(out=w1_raw[0][:], in_=w1[0:512, :].rearrange("(p j) c -> p j c", j=PACK))
         nc.sync.dma_start(offsets[:], offs)
+        nc.sync.dma_start(out=w1_raw[0][:], in_=w1[0:512, :].rearrange("(p j) c -> p j c", j=PACK))
+
+        g_win = keep.tile([P, T], F32, name="g_win", align_bytes=64)
+        nc.vector.memset(g_win[:].bitcast(I32), 0)
+        nc.sync.dma_start(out=g_win[0:1, :], in_=gate[0:1, :])
 
         xs_win = keep.tile([P, T], U8, name="xs_win", align_bytes=64)
         nc.gpsimd.memset(xs_win[:].bitcast(I32), 0)
@@ -62,33 +64,28 @@ def tile_picked_modgate_mlpsilu_p_kernel(tc, x_words, x_scales, gate, w1, w2, of
         ident = keep.tile([P, P], F32, name="ident")
         make_identity(nc, ident[:])
         out_win = keep.tile([P, T], F32, name="out_win")
-        nc.vector.memset(out_win[:], 0.0)
+        nc.vector.memset(out_win[:].bitcast(I32), 0)
 
-        g_win = keep.tile([P, T], F32, name="g_win", align_bytes=64)
-        for b in range(4):
-            gb = psum.tile([P, 4, P], F32, name="gb%d" % b, tag="acc%d" % b)
-            for c in range(4):
-                col = 4 * b + c
-                nc.tensor.transpose(gb[:, c, :], g16[:, col : col + 1].to_broadcast([P, P]), ident[:])
-            nc.vector.tensor_copy(
-                out=g_win[:].rearrange("p (n c) -> p n c", c=T // P)[:, :, 4 * b : 4 * b + 4],
-                in_=gb[:].rearrange("p c n -> p n c"),
-            )
-
-        g = keep.tile([P, S], F32, name="g")
-        nc.vector.tensor_copy(g[:], g_win[:].indirect(offsets[:]))
+        g_row = keep.tile([P, S], F32, name="g_row")
+        nc.vector.tensor_copy(g_row[:], g_win[:].indirect(offsets[:]))
 
         xs = keep.tile([P, S], U8, name="xs", tag="g_win", align_bytes=64)
         nc.vector.tensor_copy(xs[:], xs_win[:].indirect(offsets[:]))
+
+        turned = psum.tile([P, S // P, P], F32, name="turned", tag="acc0")
+        for c in range(S // P):
+            nc.tensor.transpose(turned[:, c, :], g_row[:, c * P : (c + 1) * P], ident[:])
+        g_col = keep.tile([P, S // P], F32, name="g_col")
+        nc.vector.tensor_copy(out=g_col[:], in_=turned[:, :, 0])
+        spread = psum.tile([P, S // P, P], F32, name="spread", tag="acc1")
+        for c in range(S // P):
+            nc.tensor.transpose(spread[:, c, :], g_col[:, c : c + 1].to_broadcast([P, P]), ident[:])
 
         w1_bf = []
         w1_codes = []
         w1_scales = []
         for z in range(PASSES):
-            if z == 0:
-                grouped = keep.tile([P, PACK, P, PACK], BF16, name="w1_bf0", align_bytes=64)
-            else:
-                grouped = shared.tile([P, PACK, P, PACK], BF16, name="w1_bf1", align_bytes=64, offset=0)
+            grouped = shared.tile([P, PACK, P, PACK], BF16, name="w1_bf%d" % z, align_bytes=64, offset=4096 * z)
             src = w1_raw[z][:].rearrange("p j (b t c i) -> p t b c j i", t=PACK, c=2, i=4)
             dst = grouped[:].rearrange("p t (b c i) j -> p t b c j i", c=2, i=4)
             for t in range(PACK):
@@ -108,12 +105,14 @@ def tile_picked_modgate_mlpsilu_p_kernel(tc, x_words, x_scales, gate, w1, w2, of
             w1_scales.append(scales)
 
         quantise_w1(0, "xs_win")
-        xg0 = keep.tile([P, S], U32, name="xg0", tag="w1_bf0", align_bytes=64)
+        g = keep.tile([P, S], F32, name="g", tag="w1_raw1")
+        nc.scalar.copy(out=g[:], in_=spread[:].rearrange("p c n -> p (c n)"))
+        xg0 = shared.tile([P, S], U32, name="xg0", align_bytes=64, offset=0)
         nc.vector.tensor_copy(xg0[:], x_win[0][:].bitcast(U32).indirect(offsets[:]))
         quantise_w1(1, "x_win0")
         xg1 = []
         for u in range(2):
-            picked = shared.tile([P, HALF], U32, name="xg1%d" % u, align_bytes=64, offset=4 * HALF * u)
+            picked = shared.tile([P, HALF], U32, name="xg1%d" % u, align_bytes=64, offset=4096 + 4 * HALF * u)
             nc.vector.tensor_copy(picked[:], x_win[1][:].bitcast(U32).indirect(offsets[:, 16 * u : 16 * u + 16]))
             xg1.append(picked)
 

@@ -22,23 +22,19 @@ PACK = 4
 PASSES = K // (P * PACK)
 CH = 128
 HALF = 256
+GROW = 16
 
 
 def tile_picked_modgate_mlpsilu_p_kernel(tc, x_words, x_scales, gate, w1, w2, offs, out):
     nc = tc.nc
     with ExitStack() as ctx:
         keep = ctx.enter_context(tc.tile_pool(name="keep", bufs=1))
-        shared = ctx.enter_context(tc.tile_pool(name="shared", bufs=1))
         psum = ctx.enter_context(tc.psum_pool(name="psum", bufs=1))
 
         offsets = keep.tile([P, S // 16], U16, name="offsets")
-        w1_raw = [keep.tile([P, PACK, H], F32, name="w1_raw0")]
+        w1_raw = [keep.tile([P, PACK, H], F32, name="w1_raw0", align_bytes=64)]
         nc.sync.dma_start(offsets[:], offs)
         nc.sync.dma_start(out=w1_raw[0][:], in_=w1[0:512, :].rearrange("(p j) c -> p j c", j=PACK))
-
-        g_win = keep.tile([P, T], F32, name="g_win", align_bytes=64)
-        nc.vector.memset(g_win[:].bitcast(I32), 0)
-        nc.sync.dma_start(out=g_win[0:1, :], in_=gate[0:1, :])
 
         xs_win = keep.tile([P, T], U8, name="xs_win", align_bytes=64)
         nc.gpsimd.memset(xs_win[:].bitcast(I32), 0)
@@ -48,101 +44,101 @@ def tile_picked_modgate_mlpsilu_p_kernel(tc, x_words, x_scales, gate, w1, w2, of
                 in_=x_scales[:, 4 * q : 4 * q + 4, :].bitcast(I32),
             )
 
-        warm_in = keep.tile([P, 8], F32, name="warm_in", tag="x_win0", align_bytes=64)
-        warm_out = keep.tile([P, 8], F32, name="warm_out", tag="x_win1", align_bytes=64)
-        warm_bias = keep.tile([P, 1], F32, name="warm_bias", tag="w1_raw1")
-        nc.vector.memset(warm_in[:], 0.0)
-        nc.vector.memset(warm_bias[:], 0.0)
-        nc.scalar.activation(out=warm_out[:], in_=warm_in[:], func=SILU, bias=warm_bias[:])
+        g_win = keep.tile([P, T], F32, name="g_win", align_bytes=64)
+        nc.gpsimd.memset(g_win[:, 0 : T // 2], 0.0)
+        nc.vector.memset(g_win[:, T // 2 : T].bitcast(I32), 0)
+        nc.sync.dma_start(out=g_win[GROW : GROW + 1, :], in_=gate[0:1, :])
 
-        w1_raw.append(keep.tile([P, PACK, H], F32, name="w1_raw1"))
+        ident = keep.tile([P, P], F32, name="ident")
+        make_identity(nc, ident[:])
+
+        w1_raw.append(keep.tile([P, PACK, H], F32, name="w1_raw1", align_bytes=64))
         nc.sync.dma_start(out=w1_raw[1][:], in_=w1[512:1024, :].rearrange("(p j) c -> p j c", j=PACK))
         x_win = [keep.tile([P, T], I32, name="x_win%d" % z, align_bytes=64) for z in range(PASSES)]
         for z in range(PASSES):
             nc.sync.dma_start(out=x_win[z][:], in_=x_words[z].rearrange("p n t -> p (n t)").bitcast(I32))
 
-        ident = keep.tile([P, P], F32, name="ident")
-        make_identity(nc, ident[:])
         out_win = keep.tile([P, T], F32, name="out_win")
         nc.vector.memset(out_win[:].bitcast(I32), 0)
 
-        g_row = keep.tile([P, S], F32, name="g_row")
+        xs = keep.tile([P, S], U8, name="xs", align_bytes=64)
+        nc.vector.tensor_copy(xs[:], xs_win[:].indirect(offsets[:]))
+        g_row = keep.tile([P, S], F32, name="g_row", tag="xs_win", align_bytes=64)
         nc.vector.tensor_copy(g_row[:], g_win[:].indirect(offsets[:]))
 
-        xs = keep.tile([P, S], U8, name="xs", tag="g_win", align_bytes=64)
-        nc.vector.tensor_copy(xs[:], xs_win[:].indirect(offsets[:]))
-
-        turned = psum.tile([P, S // P, P], F32, name="turned", tag="acc0")
+        turned = psum.tile([P, S // P, P], F32, name="turned")
         for c in range(S // P):
             nc.tensor.transpose(turned[:, c, :], g_row[:, c * P : (c + 1) * P], ident[:])
         g_col = keep.tile([P, S // P], F32, name="g_col")
-        nc.vector.tensor_copy(out=g_col[:], in_=turned[:, :, 0])
-        spread = psum.tile([P, S // P, P], F32, name="spread", tag="acc1")
+        nc.vector.tensor_copy(out=g_col[:], in_=turned[:, :, GROW])
+        spread = psum.tile([P, S // P, P], F32, name="spread")
         for c in range(S // P):
             nc.tensor.transpose(spread[:, c, :], g_col[:, c : c + 1].to_broadcast([P, P]), ident[:])
 
-        w1_bf = []
-        w1_codes = []
-        w1_scales = []
-        for z in range(PASSES):
-            grouped = shared.tile([P, PACK, P, PACK], BF16, name="w1_bf%d" % z, align_bytes=64, offset=4096 * z)
-            src = w1_raw[z][:].rearrange("p j (b t c i) -> p t b c j i", t=PACK, c=2, i=4)
-            dst = grouped[:].rearrange("p t (b c i) j -> p t b c j i", c=2, i=4)
-            for t in range(PACK):
-                nc.scalar.copy(out=dst[:, t], in_=src[:, t])
-            w1_bf.append(grouped)
+        w1_bf = [[], []]
+        w1_codes = [[], []]
+        w1_scales = [[], []]
 
-        w2_raw = keep.tile([P, PACK, N], F32, name="w2_raw", tag="w1_raw0")
+        def cast_w1(z, parts):
+            src = w1_raw[z][:].rearrange("p j (b t c i) -> p t b c j i", t=PACK, c=2, i=4)
+            per = PACK // parts
+            for e in range(parts):
+                grouped = keep.tile([P, per, P, PACK], BF16, name="w1_bf%d%d" % (z, e), align_bytes=64)
+                dst = grouped[:].rearrange("p t (b c i) j -> p t b c j i", c=2, i=4)
+                for t in range(per):
+                    nc.scalar.copy(out=dst[:, t], in_=src[:, per * e + t])
+                w1_bf[z].append(grouped)
+
+        def quantise_w1(z, e, tag):
+            per = PACK // len(w1_bf[z])
+            codes = keep.tile([P, per * P], U32, name="w1_codes%d%d" % (z, e), tag=tag, align_bytes=64)
+            scales = keep.tile([P, per * P], U8, name="w1_scales%d%d" % (z, e), align_bytes=64)
+            nc.vector.quantize_mx(out=codes[:].bitcast(FP8X4), scales=scales[:], in_=w1_bf[z][e][:].rearrange("p t m j -> p (t m j)"))
+            for t in range(per):
+                w1_codes[z].append(codes[:, t * P : (t + 1) * P])
+                w1_scales[z].append(scales[:, t * P : (t + 1) * P])
+
+        cast_w1(0, 1)
+        cast_w1(1, 2)
+        quantise_w1(0, 0, "g_win")
+
+        w2_raw = keep.tile([P, PACK, N], F32, name="w2_raw", align_bytes=64)
         w2_rows = w2.rearrange("(b t r) n -> t b r n", t=PACK, r=8)
         for t in range(PACK):
             nc.sync.dma_start(out=w2_raw[:, t, :], in_=w2_rows[t])
 
-        def quantise_w1(z, tag):
-            codes = keep.tile([P, H], U32, name="w1_codes%d" % z, tag=tag, align_bytes=64)
-            scales = keep.tile([P, H], U8, name="w1_scales%d" % z, align_bytes=64)
-            nc.vector.quantize_mx(out=codes[:].bitcast(FP8X4), scales=scales[:], in_=w1_bf[z][:].rearrange("p t m j -> p (t m j)"))
-            w1_codes.append(codes)
-            w1_scales.append(scales)
-
-        quantise_w1(0, "xs_win")
-        g = keep.tile([P, S], F32, name="g", tag="w1_raw1")
+        g = keep.tile([P, S], F32, name="g", tag="w1_raw1", align_bytes=64)
         nc.scalar.copy(out=g[:], in_=spread[:].rearrange("p c n -> p (c n)"))
-        xg0 = shared.tile([P, S], U32, name="xg0", align_bytes=64, offset=0)
-        nc.vector.tensor_copy(xg0[:], x_win[0][:].bitcast(U32).indirect(offsets[:]))
-        quantise_w1(1, "x_win0")
-        xg1 = []
-        for u in range(2):
-            picked = shared.tile([P, HALF], U32, name="xg1%d" % u, align_bytes=64, offset=4096 + 4 * HALF * u)
-            nc.vector.tensor_copy(picked[:], x_win[1][:].bitcast(U32).indirect(offsets[:, 16 * u : 16 * u + 16]))
-            xg1.append(picked)
+        xg = [[], []]
 
-        def first_layer(acc, c, t, z):
-            m = slice(t * P, (t + 1) * P)
-            words = xg0[:, c * CH : (c + 1) * CH] if z == 0 else xg1[c // 2][:, (c % 2) * CH : (c % 2 + 1) * CH]
-            nc.tensor.matmul_mx(
-                out=acc[:, t, :],
-                lhsT=w1_codes[z][:, m].bitcast(FP8X4),
-                lhsT_scale=w1_scales[z][:, m],
-                rhs=words.bitcast(FP8X4),
-                rhs_scale=xs[4 * z : P, c * CH : (c + 1) * CH],
-                start=(z == 0),
-                stop=(z == PASSES - 1),
-            )
+        def gather_words(z, u, tag):
+            picked = keep.tile([P, HALF], U32, name="xg%d%d" % (z, u), tag=tag, align_bytes=64)
+            nc.vector.tensor_copy(picked[:], x_win[z][:].bitcast(U32).indirect(offsets[:, 16 * u : 16 * u + 16]))
+            xg[z].append(picked)
 
-        warm_ps = psum.tile([P, 2, HALF], F32, name="warm_ps")
-        for i in range(4):
-            nc.tensor.matmul_mx(
-                out=warm_ps[:, i % 2, :],
-                lhsT=w1_codes[0][:, 0:P].bitcast(FP8X4),
-                lhsT_scale=w1_scales[0][:, 0:P],
-                rhs=xg0[:, 0:HALF].bitcast(FP8X4),
-                rhs_scale=xs[:, 0:HALF],
-                start=True,
-                stop=True,
-            )
         accs = [psum.tile([P, PACK, CH], F32, name="acc%d" % c) for c in range(S // CH)]
+
+        def first_layer(c, z):
+            words = xg[z][c // 2][:, (c % 2) * CH : (c % 2 + 1) * CH]
+            for t in range(PACK):
+                nc.tensor.matmul_mx(
+                    out=accs[c][:, t, :],
+                    lhsT=w1_codes[z][t].bitcast(FP8X4),
+                    lhsT_scale=w1_scales[z][t],
+                    rhs=words.bitcast(FP8X4),
+                    rhs_scale=xs[4 * z : P, c * CH : (c + 1) * CH],
+                    start=(z == 0 and t == 0),
+                    stop=(z == PASSES - 1 and t == PACK - 1),
+                )
+
+        for u in range(2):
+            gather_words(0, u, "xg0%d" % u)
+        quantise_w1(1, 0, "x_win0")
+        quantise_w1(1, 1, "w1_codes11")
         for c in range(S // CH):
-            first_layer(accs[c], c, 0, 0)
+            first_layer(c, 0)
+        for u in range(2):
+            gather_words(1, u, "w1_bf1%d" % u)
 
         w2_bf = keep.tile([P, N, PACK], BF16, name="w2_bf", tag="x_win1", align_bytes=64)
         nc.vector.tensor_copy(
@@ -152,26 +148,25 @@ def tile_picked_modgate_mlpsilu_p_kernel(tc, x_words, x_scales, gate, w1, w2, of
         w2_scales = keep.tile([P, N], U8, name="w2_scales", align_bytes=64)
         nc.vector.quantize_mx(out=w2_codes[:].bitcast(FP8X4), scales=w2_scales[:], in_=w2_bf[:].rearrange("p n j -> p (n j)"))
 
+        h_all = keep.tile([P, S], U32, name="h_all", tag="x_win1", align_bytes=64)
         y_ps = [psum.tile([P, HALF], F32, name="y_ps%d" % u) for u in range(2)]
         y_sb = [keep.tile([P, HALF], F32, name="y_sb%d" % u) for u in range(2)]
+        for c in range(S // CH):
+            first_layer(c, 1)
         for c in range(S // CH):
             u, v = divmod(c, 2)
             sub = slice(v * CH, (v + 1) * CH)
             acc = accs[c]
-            for t in range(PACK):
-                for z in range(PASSES):
-                    if (t, z) != (0, 0):
-                        first_layer(acc, c, t, z)
             h_bf = keep.tile([P, CH, PACK], BF16, name="h_bf%d" % c, align_bytes=64)
             nc.scalar.activation(out=h_bf[:], in_=acc[:].rearrange("p t n -> p n t"), func=SILU)
-            h_codes = keep.tile([P, CH], U32, name="h_codes%d" % c, align_bytes=64)
+            h_codes = h_all[:, c * CH : (c + 1) * CH]
             h_scales = keep.tile([P, CH], U8, name="h_scales%d" % c, align_bytes=64)
-            nc.vector.quantize_mx(out=h_codes[:].bitcast(FP8X4), scales=h_scales[:], in_=h_bf[:].rearrange("p n t -> p (n t)"))
+            nc.vector.quantize_mx(out=h_codes.bitcast(FP8X4), scales=h_scales[:], in_=h_bf[:].rearrange("p n t -> p (n t)"))
             nc.tensor.matmul_mx(
                 out=y_ps[u][:, sub],
                 lhsT=w2_codes[:].bitcast(FP8X4),
                 lhsT_scale=w2_scales[:],
-                rhs=h_codes[:].bitcast(FP8X4),
+                rhs=h_codes.bitcast(FP8X4),
                 rhs_scale=h_scales[:],
                 start=True,
                 stop=True,

@@ -33,14 +33,14 @@ def tile_picked_modgate_mlpsilu_p_kernel(tc, x_words, x_scales, gate, w1, w2, of
 
         offsets = keep.tile([P, S // 16], U16, name="offsets")
         w1_raw = [keep.tile([P, PACK, H], F32, name="w1_raw0", align_bytes=64)]
-        nc.sync.dma_start(offsets[:], offs)
         nc.sync.dma_start(out=w1_raw[0][:], in_=w1[0:512, :].rearrange("(p j) c -> p j c", j=PACK))
+        nc.sync.dma_start(offsets[:], offs)
 
         xs_win = keep.tile([P, T], U8, name="xs_win", align_bytes=64)
         nc.gpsimd.memset(xs_win[:].bitcast(I32), 0)
-        for q in range(4):
+        for q in (0, 2, 1, 3):
             nc.sync.dma_start(
-                out=xs_win[32 * q : 32 * q + 8, :].bitcast(I32),
+                out=xs_win[32 * q : 32 * q + 32 : 4, :].bitcast(I32),
                 in_=x_scales[:, 4 * q : 4 * q + 4, :].bitcast(I32),
             )
 
@@ -55,14 +55,18 @@ def tile_picked_modgate_mlpsilu_p_kernel(tc, x_words, x_scales, gate, w1, w2, of
         w1_raw.append(keep.tile([P, PACK, H], F32, name="w1_raw1", align_bytes=64))
         nc.sync.dma_start(out=w1_raw[1][:], in_=w1[512:1024, :].rearrange("(p j) c -> p j c", j=PACK))
         x_win = [keep.tile([P, T], I32, name="x_win%d" % z, align_bytes=64) for z in range(PASSES)]
-        for z in range(PASSES):
-            nc.sync.dma_start(out=x_win[z][:], in_=x_words[z].rearrange("p n t -> p (n t)").bitcast(I32))
+        nc.sync.dma_start(out=x_win[0][:], in_=x_words[0].rearrange("p n t -> p (n t)").bitcast(I32))
 
         out_win = keep.tile([P, T], F32, name="out_win")
         nc.vector.memset(out_win[:].bitcast(I32), 0)
 
+        xs_apart = keep.tile([P, S], U8, name="xs_apart", align_bytes=64)
+        nc.vector.tensor_copy(xs_apart[:], xs_win[:].indirect(offsets[:]))
         xs = keep.tile([P, S], U8, name="xs", align_bytes=64)
-        nc.vector.tensor_copy(xs[:], xs_win[:].indirect(offsets[:]))
+        nc.gpsimd.memset(xs[:].bitcast(I32), 0)
+        for q in (0, 2, 1, 3):
+            nc.sync.dma_start(out=xs[32 * q : 32 * q + 8, :].bitcast(I32), in_=xs_apart[32 * q : 32 * q + 32 : 4, :].bitcast(I32))
+        nc.sync.dma_start(out=x_win[1][:], in_=x_words[1].rearrange("p n t -> p (n t)").bitcast(I32))
         g_row = keep.tile([P, S], F32, name="g_row", tag="xs_win", align_bytes=64)
         nc.vector.tensor_copy(g_row[:], g_win[:].indirect(offsets[:]))
 

@@ -33,13 +33,13 @@ def tile_picked_modgate_mlpsilu_p_kernel(tc, x_words, x_scales, gate, w1, w2, of
 
         offsets = keep.tile([P, S // 16], U16, name="offsets")
         w1_raw = [keep.tile([P, PACK, H], F32, name="w1_raw0", align_bytes=64)]
-        nc.sync.dma_start(out=w1_raw[0][:], in_=w1[0:512, :].rearrange("(p j) c -> p j c", j=PACK))
         nc.sync.dma_start(offsets[:], offs)
+        nc.sync.dma_start(out=w1_raw[0][:], in_=w1[0:512, :].rearrange("(p j) c -> p j c", j=PACK))
 
         xs_win = keep.tile([P, T], U8, name="xs_win", align_bytes=64)
         nc.gpsimd.memset(xs_win[:].bitcast(I32), 0)
         for q in (0, 2, 1, 3):
-            nc.sync.dma_start(
+            nc.scalar.dma_start(
                 out=xs_win[32 * q : 32 * q + 32 : 4, :].bitcast(I32),
                 in_=x_scales[:, 4 * q : 4 * q + 4, :].bitcast(I32),
             )
@@ -180,4 +180,5 @@ def tile_picked_modgate_mlpsilu_p_kernel(tc, x_words, x_scales, gate, w1, w2, of
             nc.vector.tensor_tensor(
                 out_win[:].indirect(offsets[:, 16 * u : 16 * u + 16]), y_sb[u][:], g[:, u * HALF : (u + 1) * HALF], MULT
             )
-        nc.sync.dma_start(out=out, in_=out_win[:])
+        nc.sync.dma_start(out=out[:, 0 : T // 2], in_=out_win[:, 0 : T // 2])
+        nc.scalar.dma_start(out=out[:, T // 2 : T], in_=out_win[:, T // 2 : T])

@@ -33,13 +33,13 @@ def tile_picked_modgate_mlpsilu_p_kernel(tc, x_words, x_scales, gate, w1, w2, of
 
         offsets = keep.tile([P, S // 16], U16, name="offsets")
         w1_raw = [keep.tile([P, PACK, H], F32, name="w1_raw0", align_bytes=64)]
-        nc.sync.dma_start(offsets[:], offs)
         nc.sync.dma_start(out=w1_raw[0][:], in_=w1[0:512, :].rearrange("(p j) c -> p j c", j=PACK))
+        nc.sync.dma_start(offsets[:], offs)
 
         xs_win = keep.tile([P, T], U8, name="xs_win", align_bytes=64)
         nc.gpsimd.memset(xs_win[:].bitcast(I32), 0)
         for q in (0, 2, 1, 3):
-            nc.scalar.dma_start(
+            nc.sync.dma_start(
                 out=xs_win[32 * q : 32 * q + 32 : 4, :].bitcast(I32),
                 in_=x_scales[:, 4 * q : 4 * q + 4, :].bitcast(I32),
             )
@@ -84,13 +84,11 @@ def tile_picked_modgate_mlpsilu_p_kernel(tc, x_words, x_scales, gate, w1, w2, of
         w1_scales = [[], []]
 
         def cast_w1(z, parts):
-            src = w1_raw[z][:].rearrange("p j (b t c i) -> p t b c j i", t=PACK, c=2, i=4)
+            src = w1_raw[z][:].rearrange("p j (m t) -> p m j t", t=PACK)
             per = PACK // parts
             for e in range(parts):
                 grouped = keep.tile([P, per, P, PACK], BF16, name="w1_bf%d%d" % (z, e), align_bytes=64)
-                dst = grouped[:].rearrange("p t (b c i) j -> p t b c j i", c=2, i=4)
-                for t in range(per):
-                    nc.scalar.copy(out=dst[:, t], in_=src[:, per * e + t])
+                nc.scalar.copy(out=grouped[:].rearrange("p t m j -> p m j t"), in_=src[:, :, :, per * e : per * (e + 1)])
                 w1_bf[z].append(grouped)
 
         def quantise_w1(z, e, tag):
@@ -107,9 +105,7 @@ def tile_picked_modgate_mlpsilu_p_kernel(tc, x_words, x_scales, gate, w1, w2, of
         quantise_w1(0, 0, "g_win")
 
         w2_raw = keep.tile([P, PACK, N], F32, name="w2_raw", align_bytes=64)
-        w2_rows = w2.rearrange("(b t r) n -> t b r n", t=PACK, r=8)
-        for t in range(PACK):
-            nc.sync.dma_start(out=w2_raw[:, t, :], in_=w2_rows[t])
+        nc.sync.dma_start(out=w2_raw[:], in_=w2.rearrange("(p j) n -> p j n", j=PACK))
 
         g = keep.tile([P, S], F32, name="g", tag="w1_raw1", align_bytes=64)
         nc.scalar.copy(out=g[:], in_=spread[:].rearrange("p c n -> p (c n)"))
@@ -153,21 +149,29 @@ def tile_picked_modgate_mlpsilu_p_kernel(tc, x_words, x_scales, gate, w1, w2, of
         nc.vector.quantize_mx(out=w2_codes[:].bitcast(FP8X4), scales=w2_scales[:], in_=w2_bf[:].rearrange("p n j -> p (n j)"))
 
         h_all = keep.tile([P, S], U32, name="h_all", tag="x_win1", align_bytes=64)
-        y_ps = [psum.tile([P, HALF], F32, name="y_ps%d" % u) for u in range(2)]
-        y_sb = [keep.tile([P, HALF], F32, name="y_sb%d" % u) for u in range(2)]
+        y_late = psum.tile([P, HALF], F32, name="y_late")
+        y_ps = [
+            psum.tile([P, CH], F32, name="y_ps0", tag="turned")[:],
+            psum.tile([P, CH], F32, name="y_ps1", tag="spread")[:],
+            y_late[:, 0:CH],
+            y_late[:, CH:HALF],
+        ]
+        y_sb = []
         for c in range(S // CH):
             first_layer(c, 1)
         for c in range(S // CH):
-            u, v = divmod(c, 2)
-            sub = slice(v * CH, (v + 1) * CH)
             acc = accs[c]
             h_bf = keep.tile([P, CH, PACK], BF16, name="h_bf%d" % c, align_bytes=64)
             nc.scalar.activation(out=h_bf[:], in_=acc[:].rearrange("p t n -> p n t"), func=SILU)
+            if c == 2:
+                y_sb.append(keep.tile([P, HALF], F32, name="y_sb0", tag="h_bf1", align_bytes=64))
+                y_sb.append(keep.tile([P, HALF], F32, name="y_sb1"))
+                nc.vector.tensor_copy(out=y_sb[0][:, 0:CH], in_=y_ps[0])
             h_codes = h_all[:, c * CH : (c + 1) * CH]
             h_scales = keep.tile([P, CH], U8, name="h_scales%d" % c, align_bytes=64)
             nc.vector.quantize_mx(out=h_codes.bitcast(FP8X4), scales=h_scales[:], in_=h_bf[:].rearrange("p n t -> p (n t)"))
             nc.tensor.matmul_mx(
-                out=y_ps[u][:, sub],
+                out=y_ps[c],
                 lhsT=w2_codes[:].bitcast(FP8X4),
                 lhsT_scale=w2_scales[:],
                 rhs=h_codes.bitcast(FP8X4),
@@ -175,10 +179,10 @@ def tile_picked_modgate_mlpsilu_p_kernel(tc, x_words, x_scales, gate, w1, w2, of
                 start=True,
                 stop=True,
             )
+        nc.scalar.copy(out=y_sb[0][:, CH:HALF], in_=y_ps[1])
+        nc.scalar.copy(out=y_sb[1][:], in_=y_late[:])
         for u in range(2):
-            nc.scalar.copy(out=y_sb[u][:], in_=y_ps[u][:])
             nc.vector.tensor_tensor(
                 out_win[:].indirect(offsets[:, 16 * u : 16 * u + 16]), y_sb[u][:], g[:, u * HALF : (u + 1) * HALF], MULT
             )
-        nc.sync.dma_start(out=out[:, 0 : T // 2], in_=out_win[:, 0 : T // 2])
-        nc.scalar.dma_start(out=out[:, T // 2 : T], in_=out_win[:, T // 2 : T])
+        nc.sync.dma_start(out=out, in_=out_win[:])

@@ -22,7 +22,7 @@ PACK = 4
 PASSES = K // (P * PACK)
 CH = 128
 HALF = 256
-GROW = 16
+GROW = 4
 
 
 def tile_picked_modgate_mlpsilu_p_kernel(tc, x_words, x_scales, gate, w1, w2, offs, out):
@@ -33,16 +33,15 @@ def tile_picked_modgate_mlpsilu_p_kernel(tc, x_words, x_scales, gate, w1, w2, of
 
         offsets = keep.tile([P, S // 16], U16, name="offsets")
         w1_raw = [keep.tile([P, PACK, H], F32, name="w1_raw0", align_bytes=64)]
-        nc.sync.dma_start(out=w1_raw[0][:], in_=w1[0:512, :].rearrange("(p j) c -> p j c", j=PACK))
+        w1_first = w1[0:512, :].rearrange("(p j) c -> p j c", j=PACK)
+        nc.sync.dma_start(out=w1_raw[0][:, 0:2, :], in_=w1_first[:, 0:2, :])
         nc.sync.dma_start(offsets[:], offs)
 
-        xs_win = keep.tile([P, T], U8, name="xs_win", align_bytes=64)
+        xs_win = keep.tile([P, PASSES, T], U8, name="xs_win", align_bytes=64)
         nc.gpsimd.memset(xs_win[:].bitcast(I32), 0)
-        for q in (0, 2, 1, 3):
-            nc.sync.dma_start(
-                out=xs_win[32 * q : 32 * q + 32 : 4, :].bitcast(I32),
-                in_=x_scales[:, 4 * q : 4 * q + 4, :].bitcast(I32),
-            )
+        nc.sync.dma_start(out=xs_win[0:P:8, :, :].bitcast(I32), in_=x_scales.rearrange("z r c -> r z c").bitcast(I32))
+
+        nc.sync.dma_start(out=w1_raw[0][:, 2:4, :], in_=w1_first[:, 2:4, :])
 
         g_win = keep.tile([P, T], F32, name="g_win", align_bytes=64)
         nc.gpsimd.memset(g_win[:, 0 : T // 2], 0.0)
@@ -58,14 +57,18 @@ def tile_picked_modgate_mlpsilu_p_kernel(tc, x_words, x_scales, gate, w1, w2, of
         nc.sync.dma_start(out=x_win[0][:], in_=x_words[0].rearrange("p n t -> p (n t)").bitcast(I32))
 
         out_win = keep.tile([P, T], F32, name="out_win")
-        nc.vector.memset(out_win[:].bitcast(I32), 0)
+        zero = keep.tile([P, 1], F32, name="zero")
+        nc.vector.memset(zero[:], 0.0)
+        nc.scalar.activation(out=out_win[:, 0 : T // 2], in_=zero[:].to_broadcast([P, T // 2]), func=SILU)
+        nc.vector.memset(out_win[:, T // 2 : T].bitcast(I32), 0)
 
-        xs_apart = keep.tile([P, S], U8, name="xs_apart", align_bytes=64)
-        nc.vector.tensor_copy(xs_apart[:], xs_win[:].indirect(offsets[:]))
-        xs = keep.tile([P, S], U8, name="xs", align_bytes=64)
+        xs_apart = keep.tile([P, PASSES * S], U8, name="xs_apart", align_bytes=64)
+        for z in range(PASSES):
+            nc.vector.tensor_copy(xs_apart[:, z * S : (z + 1) * S], xs_win[:, z, :].indirect(offsets[:]))
+        xs = keep.tile([P, PASSES * S], U8, name="xs", align_bytes=64)
         nc.gpsimd.memset(xs[:].bitcast(I32), 0)
         for q in (0, 2, 1, 3):
-            nc.sync.dma_start(out=xs[32 * q : 32 * q + 8, :].bitcast(I32), in_=xs_apart[32 * q : 32 * q + 32 : 4, :].bitcast(I32))
+            nc.sync.dma_start(out=xs[32 * q : 32 * q + 4, :].bitcast(I32), in_=xs_apart[32 * q : 32 * q + 32 : 8, :].bitcast(I32))
         nc.sync.dma_start(out=x_win[1][:], in_=x_words[1].rearrange("p n t -> p (n t)").bitcast(I32))
         g_row = keep.tile([P, S], F32, name="g_row", tag="xs_win", align_bytes=64)
         nc.vector.tensor_copy(g_row[:], g_win[:].indirect(offsets[:]))
@@ -126,7 +129,7 @@ def tile_picked_modgate_mlpsilu_p_kernel(tc, x_words, x_scales, gate, w1, w2, of
                     lhsT=w1_codes[z][t].bitcast(FP8X4),
                     lhsT_scale=w1_scales[z][t],
                     rhs=words.bitcast(FP8X4),
-                    rhs_scale=xs[4 * z : P, c * CH : (c + 1) * CH],
+                    rhs_scale=xs[:, z * S + c * CH : z * S + (c + 1) * CH],
                     start=(z == 0 and t == 0),
                     stop=(z == PASSES - 1 and t == PACK - 1),
                 )

@@ -32,45 +32,44 @@ def tile_picked_modgate_mlpsilu_p_kernel(tc, x_words, x_scales, gate, w1, w2, of
         psum = ctx.enter_context(tc.psum_pool(name="psum", bufs=1))
 
         offsets = keep.tile([P, S // 16], U16, name="offsets")
-        w1_raw = [keep.tile([P, PACK, H], F32, name="w1_raw0", align_bytes=64)]
-        w1_first = w1[0:512, :].rearrange("(p j) c -> p j c", j=PACK)
-        nc.sync.dma_start(out=w1_raw[0][:, 0:2, :], in_=w1_first[:, 0:2, :])
+        w1_raw = [keep.tile([P, PACK, H], F32, name="w1_raw%d" % z, align_bytes=64) for z in range(PASSES)]
+        w1_rows = w1.rearrange("(z p j) c -> z p j c", z=PASSES, j=PACK)
+        nc.sync.dma_start(out=w1_raw[0][:, 0:2, :], in_=w1_rows[0, :, 0:2, :])
         nc.sync.dma_start(offsets[:], offs)
 
         xs_win = keep.tile([P, PASSES, T], U8, name="xs_win", align_bytes=64)
-        nc.gpsimd.memset(xs_win[:].bitcast(I32), 0)
+        nc.vector.memset(xs_win[:].bitcast(I32), 0)
         nc.sync.dma_start(out=xs_win[0:P:8, :, :].bitcast(I32), in_=x_scales.rearrange("z r c -> r z c").bitcast(I32))
-
-        nc.sync.dma_start(out=w1_raw[0][:, 2:4, :], in_=w1_first[:, 2:4, :])
+        nc.sync.dma_start(out=w1_raw[0][:, 2:4, :], in_=w1_rows[0, :, 2:4, :])
+        nc.sync.dma_start(out=w1_raw[1][:, 0:2, :], in_=w1_rows[1, :, 0:2, :])
 
         g_win = keep.tile([P, T], F32, name="g_win", align_bytes=64)
-        nc.gpsimd.memset(g_win[:, 0 : T // 2], 0.0)
-        nc.vector.memset(g_win[:, T // 2 : T].bitcast(I32), 0)
+        nc.vector.memset(g_win[:].bitcast(I32), 0)
         nc.sync.dma_start(out=g_win[GROW : GROW + 1, :], in_=gate[0:1, :])
+        nc.sync.dma_start(out=w1_raw[1][:, 2:4, :], in_=w1_rows[1, :, 2:4, :])
 
         ident = keep.tile([P, P], F32, name="ident")
-        make_identity(nc, ident[:])
+        nc.vector.memset(ident[:], 0.0)
+        make_identity(nc, ident[:], nomemset=True)
 
-        w1_raw.append(keep.tile([P, PACK, H], F32, name="w1_raw1", align_bytes=64))
-        nc.sync.dma_start(out=w1_raw[1][:], in_=w1[512:1024, :].rearrange("(p j) c -> p j c", j=PACK))
-        x_win = [keep.tile([P, T], I32, name="x_win%d" % z, align_bytes=64) for z in range(PASSES)]
+        x_win = [keep.tile([P, T], I32, name="x_win0", align_bytes=64)]
         nc.sync.dma_start(out=x_win[0][:], in_=x_words[0].rearrange("p n t -> p (n t)").bitcast(I32))
 
+        xs = keep.tile([P, PASSES * S], U8, name="xs", align_bytes=64)
+        nc.vector.memset(xs[:].bitcast(I32), 0)
         out_win = keep.tile([P, T], F32, name="out_win")
         zero = keep.tile([P, 1], F32, name="zero")
-        nc.vector.memset(zero[:], 0.0)
-        nc.scalar.activation(out=out_win[:, 0 : T // 2], in_=zero[:].to_broadcast([P, T // 2]), func=SILU)
-        nc.vector.memset(out_win[:, T // 2 : T].bitcast(I32), 0)
+        nc.gpsimd.memset(zero[:], 0.0)
+        nc.scalar.activation(out=out_win[:], in_=zero[:].to_broadcast([P, T]), func=SILU)
 
         xs_apart = keep.tile([P, PASSES * S], U8, name="xs_apart", align_bytes=64)
         for z in range(PASSES):
             nc.vector.tensor_copy(xs_apart[:, z * S : (z + 1) * S], xs_win[:, z, :].indirect(offsets[:]))
-        xs = keep.tile([P, PASSES * S], U8, name="xs", align_bytes=64)
-        nc.gpsimd.memset(xs[:].bitcast(I32), 0)
         for q in (0, 2, 1, 3):
             nc.sync.dma_start(out=xs[32 * q : 32 * q + 4, :].bitcast(I32), in_=xs_apart[32 * q : 32 * q + 32 : 8, :].bitcast(I32))
+        x_win.append(keep.tile([P, T], I32, name="x_win1", tag="xs_win", align_bytes=64))
         nc.sync.dma_start(out=x_win[1][:], in_=x_words[1].rearrange("p n t -> p (n t)").bitcast(I32))
-        g_row = keep.tile([P, S], F32, name="g_row", tag="xs_win", align_bytes=64)
+        g_row = keep.tile([P, S], F32, name="g_row", align_bytes=64)
         nc.vector.tensor_copy(g_row[:], g_win[:].indirect(offsets[:]))
 
         turned = psum.tile([P, S // P, P], F32, name="turned")
@@ -107,7 +106,7 @@ def tile_picked_modgate_mlpsilu_p_kernel(tc, x_words, x_scales, gate, w1, w2, of
         cast_w1(1, 2)
         quantise_w1(0, 0, "g_win")
 
-        w2_raw = keep.tile([P, PACK, N], F32, name="w2_raw", align_bytes=64)
+        w2_raw = keep.tile([P, PACK, N], F32, name="w2_raw", tag="xs_apart", align_bytes=64)
         nc.sync.dma_start(out=w2_raw[:], in_=w2.rearrange("(p j) n -> p j n", j=PACK))
 
         g = keep.tile([P, S], F32, name="g", tag="w1_raw1", align_bytes=64)
@@ -135,15 +134,15 @@ def tile_picked_modgate_mlpsilu_p_kernel(tc, x_words, x_scales, gate, w1, w2, of
                 )
 
         for u in range(2):
-            gather_words(0, u, "xg0%d" % u)
-        quantise_w1(1, 0, "x_win0")
-        quantise_w1(1, 1, "w1_codes11")
+            gather_words(0, u, "g_row" if u == 0 else "xg01")
+        quantise_w1(1, 0, "w1_codes10")
+        quantise_w1(1, 1, "x_win0")
         for c in range(S // CH):
             first_layer(c, 0)
         for u in range(2):
             gather_words(1, u, "w1_bf1%d" % u)
 
-        w2_bf = keep.tile([P, N, PACK], BF16, name="w2_bf", tag="x_win1", align_bytes=64)
+        w2_bf = keep.tile([P, N, PACK], BF16, name="w2_bf", tag="xs_win", align_bytes=64)
         nc.vector.tensor_copy(
             out=w2_bf[:].rearrange("p (c i) j -> p c j i", i=4), in_=w2_raw[:].rearrange("p j (c i) -> p c j i", i=4)
         )
@@ -151,7 +150,7 @@ def tile_picked_modgate_mlpsilu_p_kernel(tc, x_words, x_scales, gate, w1, w2, of
         w2_scales = keep.tile([P, N], U8, name="w2_scales", align_bytes=64)
         nc.vector.quantize_mx(out=w2_codes[:].bitcast(FP8X4), scales=w2_scales[:], in_=w2_bf[:].rearrange("p n j -> p (n j)"))
 
-        h_all = keep.tile([P, S], U32, name="h_all", tag="x_win1", align_bytes=64)
+        h_all = keep.tile([P, S], U32, name="h_all", tag="xs_win", align_bytes=64)
         y_late = psum.tile([P, HALF], F32, name="y_late")
         y_ps = [
             psum.tile([P, CH], F32, name="y_ps0", tag="turned")[:],

@@ -22,7 +22,7 @@ PACK = 4
 PASSES = K // (P * PACK)
 CH = 128
 HALF = 256
-GROW = 4
+GROW = 8
 
 
 def tile_picked_modgate_mlpsilu_p_kernel(tc, x_words, x_scales, gate, w1, w2, offs, out):
@@ -39,7 +39,7 @@ def tile_picked_modgate_mlpsilu_p_kernel(tc, x_words, x_scales, gate, w1, w2, of
 
         xs_win = keep.tile([P, PASSES, T], U8, name="xs_win", align_bytes=64)
         nc.vector.memset(xs_win[:].bitcast(I32), 0)
-        nc.sync.dma_start(out=xs_win[0:P:8, :, :].bitcast(I32), in_=x_scales.rearrange("z r c -> r z c").bitcast(I32))
+        nc.sync.dma_start(out=xs_win[4:P:8, :, :].bitcast(I32), in_=x_scales.rearrange("z r c -> r z c").bitcast(I32))
         nc.sync.dma_start(out=w1_raw[0][:, 2:4, :], in_=w1_rows[0, :, 2:4, :])
         nc.sync.dma_start(out=w1_raw[1][:, 0:2, :], in_=w1_rows[1, :, 0:2, :])
 
@@ -66,7 +66,7 @@ def tile_picked_modgate_mlpsilu_p_kernel(tc, x_words, x_scales, gate, w1, w2, of
         for z in range(PASSES):
             nc.vector.tensor_copy(xs_apart[:, z * S : (z + 1) * S], xs_win[:, z, :].indirect(offsets[:]))
         for q in (0, 2, 1, 3):
-            nc.sync.dma_start(out=xs[32 * q : 32 * q + 4, :].bitcast(I32), in_=xs_apart[32 * q : 32 * q + 32 : 8, :].bitcast(I32))
+            nc.sync.dma_start(out=xs[32 * q : 32 * q + 4, :].bitcast(I32), in_=xs_apart[32 * q + 4 : 32 * q + 32 : 8, :].bitcast(I32))
         x_win.append(keep.tile([P, T], I32, name="x_win1", tag="xs_win", align_bytes=64))
         nc.sync.dma_start(out=x_win[1][:], in_=x_words[1].rearrange("p n t -> p (n t)").bitcast(I32))
         g_row = keep.tile([P, S], F32, name="g_row", align_bytes=64)
@@ -142,15 +142,15 @@ def tile_picked_modgate_mlpsilu_p_kernel(tc, x_words, x_scales, gate, w1, w2, of
         for u in range(2):
             gather_words(1, u, "w1_bf1%d" % u)
 
-        w2_bf = keep.tile([P, N, PACK], BF16, name="w2_bf", tag="xs_win", align_bytes=64)
-        nc.vector.tensor_copy(
+        w2_bf = keep.tile([P, N, PACK], BF16, name="w2_bf", align_bytes=64)
+        nc.scalar.copy(
             out=w2_bf[:].rearrange("p (c i) j -> p c j i", i=4), in_=w2_raw[:].rearrange("p j (c i) -> p c j i", i=4)
         )
-        w2_codes = keep.tile([P, N], U32, name="w2_codes", align_bytes=64)
+        w2_codes = keep.tile([P, N], U32, name="w2_codes", tag="xs_win", align_bytes=64)
         w2_scales = keep.tile([P, N], U8, name="w2_scales", align_bytes=64)
         nc.vector.quantize_mx(out=w2_codes[:].bitcast(FP8X4), scales=w2_scales[:], in_=w2_bf[:].rearrange("p n j -> p (n j)"))
 
-        h_all = keep.tile([P, S], U32, name="h_all", tag="xs_win", align_bytes=64)
+        h_all = keep.tile([P, S], U32, name="h_all", tag="w2_bf", align_bytes=64)
         y_late = psum.tile([P, HALF], F32, name="y_late")
         y_ps = [
             psum.tile([P, CH], F32, name="y_ps0", tag="turned")[:],

@@ -16,6 +16,7 @@ U8 = mybir.dt.uint8
 FP8X4 = mybir.dt.float8_e4m3fn_x4
 SILU = mybir.ActivationFunctionType.Silu
 MULT = mybir.AluOpType.mult
+ADD = mybir.AluOpType.add
 
 P = 128
 PACK = 4
@@ -23,6 +24,7 @@ PASSES = K // (P * PACK)
 CH = 128
 HALF = 256
 GROW = 8
+FIRST = 64
 
 
 def tile_picked_modgate_mlpsilu_p_kernel(tc, x_words, x_scales, gate, w1, w2, offs, out):
@@ -55,19 +57,18 @@ def tile_picked_modgate_mlpsilu_p_kernel(tc, x_words, x_scales, gate, w1, w2, of
         x_win = [keep.tile([P, T], I32, name="x_win0", align_bytes=64)]
         nc.sync.dma_start(out=x_win[0][:], in_=x_words[0].rearrange("p n t -> p (n t)").bitcast(I32))
 
-        xs = keep.tile([P, PASSES * S], U8, name="xs", align_bytes=64)
-        nc.vector.memset(xs[:].bitcast(I32), 0)
         out_win = keep.tile([P, T], F32, name="out_win")
-        zero = keep.tile([P, 1], F32, name="zero")
+        zero = keep.tile([P, CH], F32, name="zero")
         nc.gpsimd.memset(zero[:], 0.0)
-        nc.scalar.activation(out=out_win[:], in_=zero[:].to_broadcast([P, T]), func=SILU)
+        nc.scalar.activation(out=out_win[:], in_=zero[:, 0:1].to_broadcast([P, T]), func=SILU)
 
         xs_apart = keep.tile([P, PASSES * S], U8, name="xs_apart", align_bytes=64)
         for z in range(PASSES):
             nc.vector.tensor_copy(xs_apart[:, z * S : (z + 1) * S], xs_win[:, z, :].indirect(offsets[:]))
+        xs = keep.tile([P, PASSES * S], U8, name="xs", tag="xs_win", align_bytes=64)
         for q in (0, 2, 1, 3):
             nc.sync.dma_start(out=xs[32 * q : 32 * q + 4, :].bitcast(I32), in_=xs_apart[32 * q + 4 : 32 * q + 32 : 8, :].bitcast(I32))
-        x_win.append(keep.tile([P, T], I32, name="x_win1", tag="xs_win", align_bytes=64))
+        x_win.append(keep.tile([P, T], I32, name="x_win1", align_bytes=64))
         nc.sync.dma_start(out=x_win[1][:], in_=x_words[1].rearrange("p n t -> p (n t)").bitcast(I32))
         g_row = keep.tile([P, S], F32, name="g_row", align_bytes=64)
         nc.vector.tensor_copy(g_row[:], g_win[:].indirect(offsets[:]))
@@ -146,34 +147,27 @@ def tile_picked_modgate_mlpsilu_p_kernel(tc, x_words, x_scales, gate, w1, w2, of
         nc.scalar.copy(
             out=w2_bf[:].rearrange("p (c i) j -> p c j i", i=4), in_=w2_raw[:].rearrange("p j (c i) -> p c j i", i=4)
         )
-        w2_codes = keep.tile([P, N], U32, name="w2_codes", tag="xs_win", align_bytes=64)
+        w2_codes = keep.tile([P, N], U32, name="w2_codes", tag="x_win1", align_bytes=64)
         w2_scales = keep.tile([P, N], U8, name="w2_scales", align_bytes=64)
         nc.vector.quantize_mx(out=w2_codes[:].bitcast(FP8X4), scales=w2_scales[:], in_=w2_bf[:].rearrange("p n j -> p (n j)"))
 
-        h_all = keep.tile([P, S], U32, name="h_all", tag="w2_bf", align_bytes=64)
-        y_late = psum.tile([P, HALF], F32, name="y_late")
-        y_ps = [
-            psum.tile([P, CH], F32, name="y_ps0", tag="turned")[:],
-            psum.tile([P, CH], F32, name="y_ps1", tag="spread")[:],
-            y_late[:, 0:CH],
-            y_late[:, CH:HALF],
-        ]
-        y_sb = []
+        h_all = keep.tile([P, S], U32, name="h_all", align_bytes=64)
+        y_first = psum.tile([P, FIRST], F32, name="y_first", tag="turned")
+        y_second = psum.tile([P, FIRST], F32, name="y_second", tag="spread")
+        y_third = psum.tile([P, CH], F32, name="y_third", tag="acc2")
+        y_late = [psum.tile([P, CH], F32, name="y_late%d" % i) for i in range(2)]
         for c in range(S // CH):
             first_layer(c, 1)
-        for c in range(S // CH):
-            acc = accs[c]
-            h_bf = keep.tile([P, CH, PACK], BF16, name="h_bf%d" % c, align_bytes=64)
-            nc.scalar.activation(out=h_bf[:], in_=acc[:].rearrange("p t n -> p n t"), func=SILU)
-            if c == 2:
-                y_sb.append(keep.tile([P, HALF], F32, name="y_sb0", tag="h_bf1", align_bytes=64))
-                y_sb.append(keep.tile([P, HALF], F32, name="y_sb1"))
-                nc.vector.tensor_copy(out=y_sb[0][:, 0:CH], in_=y_ps[0])
-            h_codes = h_all[:, c * CH : (c + 1) * CH]
-            h_scales = keep.tile([P, CH], U8, name="h_scales%d" % c, align_bytes=64)
+
+        def hidden(lo, hi, y_ps):
+            acc = accs[lo // CH][:, :, lo % CH : lo % CH + hi - lo]
+            h_bf = keep.tile([P, hi - lo, PACK], BF16, name="h_bf%d" % lo, align_bytes=64)
+            nc.scalar.activation(out=h_bf[:], in_=acc.rearrange("p t n -> p n t"), func=SILU)
+            h_codes = h_all[:, lo:hi]
+            h_scales = keep.tile([P, hi - lo], U8, name="h_scales%d" % lo, align_bytes=64)
             nc.vector.quantize_mx(out=h_codes.bitcast(FP8X4), scales=h_scales[:], in_=h_bf[:].rearrange("p n t -> p (n t)"))
             nc.tensor.matmul_mx(
-                out=y_ps[c],
+                out=y_ps,
                 lhsT=w2_codes[:].bitcast(FP8X4),
                 lhsT_scale=w2_scales[:],
                 rhs=h_codes.bitcast(FP8X4),
@@ -181,10 +175,32 @@ def tile_picked_modgate_mlpsilu_p_kernel(tc, x_words, x_scales, gate, w1, w2, of
                 start=True,
                 stop=True,
             )
-        nc.scalar.copy(out=y_sb[0][:, CH:HALF], in_=y_ps[1])
-        nc.scalar.copy(out=y_sb[1][:], in_=y_late[:])
-        for u in range(2):
-            nc.vector.tensor_tensor(
-                out_win[:].indirect(offsets[:, 16 * u : 16 * u + 16]), y_sb[u][:], g[:, u * HALF : (u + 1) * HALF], MULT
-            )
+
+        def weigh(lo, hi, y_ps):
+            yg = keep.tile([P, hi - lo], F32, name="yg%d" % lo)
+            nc.vector.tensor_tensor(yg[:], y_ps, g[:, lo:hi], MULT)
+            return yg
+
+        def place(lo, hi, yg, zeros):
+            nc.vector.tensor_tensor(out_win[:].indirect(offsets[:, lo // 16 : hi // 16]), yg[:], zeros, ADD)
+
+        hidden(0, FIRST, y_first[:])
+        hidden(FIRST, CH, y_second[:])
+        yg_first = weigh(0, FIRST, y_first[:])
+        hidden(CH, HALF, y_third[:])
+        yg_second = weigh(FIRST, CH, y_second[:])
+        zeros_first = keep.tile([P, FIRST], F32, name="zeros_first", tag="h_bf%d" % FIRST, align_bytes=64)
+        nc.scalar.copy(out=zeros_first[:], in_=zero[:, 0:1].to_broadcast([P, FIRST]))
+        place(0, FIRST, yg_first, zeros_first[:])
+        hidden(HALF, HALF + CH, y_late[0][:])
+        zeros_second = keep.tile([P, FIRST], F32, name="zeros_second", tag="h_bf%d" % CH, align_bytes=64)
+        nc.scalar.copy(out=zeros_second[:], in_=zero[:, 0:1].to_broadcast([P, FIRST]))
+        place(FIRST, CH, yg_second, zeros_second[:])
+        yg_third = weigh(CH, HALF, y_third[:])
+        hidden(HALF + CH, S, y_late[1][:])
+        place(CH, HALF, yg_third, zero[:])
+        y_sb = keep.tile([P, HALF], F32, name="y_sb")
+        for i in range(2):
+            nc.scalar.copy(out=y_sb[:, i * CH : (i + 1) * CH], in_=y_late[i][:])
+        nc.vector.tensor_tensor(out_win[:].indirect(offsets[:, HALF // 16 : S // 16]), y_sb[:], g[:, HALF:S], MULT)
         nc.sync.dma_start(out=out, in_=out_win[:])

@@ -154,7 +154,7 @@ def tile_picked_modgate_mlpsilu_p_kernel(tc, x_words, x_scales, gate, w1, w2, of
         h_all = keep.tile([P, S], U32, name="h_all", align_bytes=64)
         y_first = psum.tile([P, FIRST], F32, name="y_first", tag="turned")
         y_second = psum.tile([P, FIRST], F32, name="y_second", tag="spread")
-        y_third = psum.tile([P, CH], F32, name="y_third", tag="acc2")
+        y_last = psum.tile([P, CH], F32, name="y_last", tag="acc0")
         y_late = [psum.tile([P, CH], F32, name="y_late%d" % i) for i in range(2)]
         for c in range(S // CH):
             first_layer(c, 1)
@@ -187,20 +187,20 @@ def tile_picked_modgate_mlpsilu_p_kernel(tc, x_words, x_scales, gate, w1, w2, of
         hidden(0, FIRST, y_first[:])
         hidden(FIRST, CH, y_second[:])
         yg_first = weigh(0, FIRST, y_first[:])
-        hidden(CH, HALF, y_third[:])
+        hidden(CH, HALF, y_late[0][:])
         yg_second = weigh(FIRST, CH, y_second[:])
         zeros_first = keep.tile([P, FIRST], F32, name="zeros_first", tag="h_bf%d" % FIRST, align_bytes=64)
         nc.scalar.copy(out=zeros_first[:], in_=zero[:, 0:1].to_broadcast([P, FIRST]))
         place(0, FIRST, yg_first, zeros_first[:])
-        hidden(HALF, HALF + CH, y_late[0][:])
+        hidden(HALF, HALF + CH, y_late[1][:])
         zeros_second = keep.tile([P, FIRST], F32, name="zeros_second", tag="h_bf%d" % CH, align_bytes=64)
         nc.scalar.copy(out=zeros_second[:], in_=zero[:, 0:1].to_broadcast([P, FIRST]))
         place(FIRST, CH, yg_second, zeros_second[:])
-        yg_third = weigh(CH, HALF, y_third[:])
-        hidden(HALF + CH, S, y_late[1][:])
-        place(CH, HALF, yg_third, zero[:])
+        hidden(HALF + CH, S, y_last[:])
         y_sb = keep.tile([P, HALF], F32, name="y_sb")
         for i in range(2):
             nc.scalar.copy(out=y_sb[:, i * CH : (i + 1) * CH], in_=y_late[i][:])
-        nc.vector.tensor_tensor(out_win[:].indirect(offsets[:, HALF // 16 : S // 16]), y_sb[:], g[:, HALF:S], MULT)
+        nc.vector.tensor_tensor(out_win[:].indirect(offsets[:, CH // 16 : (CH + HALF) // 16]), y_sb[:], g[:, CH : CH + HALF], MULT)
+        yg_last = weigh(HALF + CH, S, y_last[:])
+        place(HALF + CH, S, yg_last, zero[:])
         nc.sync.dma_start(out=out, in_=out_win[:])

@@ -154,8 +154,8 @@ def tile_picked_modgate_mlpsilu_p_kernel(tc, x_words, x_scales, gate, w1, w2, of
         h_all = keep.tile([P, S], U32, name="h_all", align_bytes=64)
         y_first = psum.tile([P, FIRST], F32, name="y_first", tag="turned")
         y_second = psum.tile([P, FIRST], F32, name="y_second", tag="spread")
-        y_last = psum.tile([P, CH], F32, name="y_last", tag="acc0")
-        y_late = [psum.tile([P, CH], F32, name="y_late%d" % i) for i in range(2)]
+        y_mid = psum.tile([P, HALF], F32, name="y_mid")
+        y_last = psum.tile([P, CH], F32, name="y_last")
         for c in range(S // CH):
             first_layer(c, 1)
 
@@ -187,20 +187,17 @@ def tile_picked_modgate_mlpsilu_p_kernel(tc, x_words, x_scales, gate, w1, w2, of
         hidden(0, FIRST, y_first[:])
         hidden(FIRST, CH, y_second[:])
         yg_first = weigh(0, FIRST, y_first[:])
-        hidden(CH, HALF, y_late[0][:])
+        hidden(CH, HALF, y_mid[:, :CH])
         yg_second = weigh(FIRST, CH, y_second[:])
-        zeros_first = keep.tile([P, FIRST], F32, name="zeros_first", tag="h_bf%d" % FIRST, align_bytes=64)
-        nc.scalar.copy(out=zeros_first[:], in_=zero[:, 0:1].to_broadcast([P, FIRST]))
-        place(0, FIRST, yg_first, zeros_first[:])
-        hidden(HALF, HALF + CH, y_late[1][:])
-        zeros_second = keep.tile([P, FIRST], F32, name="zeros_second", tag="h_bf%d" % CH, align_bytes=64)
+        place(0, FIRST, yg_first, zero[:, :FIRST])
+        hidden(HALF, HALF + CH, y_mid[:, CH:])
+        hidden(HALF + CH, S - FIRST, y_last[:, :FIRST])
+        hidden(S - FIRST, S, y_last[:, FIRST:])
+        zeros_second = keep.tile([P, FIRST], F32, name="zeros_second", tag="h_bf%d" % HALF, align_bytes=64)
         nc.scalar.copy(out=zeros_second[:], in_=zero[:, 0:1].to_broadcast([P, FIRST]))
         place(FIRST, CH, yg_second, zeros_second[:])
-        hidden(HALF + CH, S, y_last[:])
-        y_sb = keep.tile([P, HALF], F32, name="y_sb")
-        for i in range(2):
-            nc.scalar.copy(out=y_sb[:, i * CH : (i + 1) * CH], in_=y_late[i][:])
-        nc.vector.tensor_tensor(out_win[:].indirect(offsets[:, CH // 16 : (CH + HALF) // 16]), y_sb[:], g[:, CH : CH + HALF], MULT)
-        yg_last = weigh(HALF + CH, S, y_last[:])
-        place(HALF + CH, S, yg_last, zero[:])
+        y_sb = keep.tile([P, S - CH], F32, name="y_sb")
+        nc.scalar.copy(out=y_sb[:, :HALF], in_=y_mid[:])
+        nc.scalar.copy(out=y_sb[:, HALF:], in_=y_last[:])
+        nc.vector.tensor_tensor(out_win[:].indirect(offsets[:, CH // 16 : S // 16]), y_sb[:], g[:, CH:S], MULT)
         nc.sync.dma_start(out=out, in_=out_win[:])

@@ -15,6 +15,7 @@ U16 = mybir.dt.uint16
 U8 = mybir.dt.uint8
 FP8X4 = mybir.dt.float8_e4m3fn_x4
 SILU = mybir.ActivationFunctionType.Silu
+COPY = mybir.ActivationFunctionType.Copy
 MULT = mybir.AluOpType.mult
 ADD = mybir.AluOpType.add
 
@@ -31,6 +32,7 @@ def tile_picked_modgate_mlpsilu_p_kernel(tc, x_words, x_scales, gate, w1, w2, of
     nc = tc.nc
     with ExitStack() as ctx:
         keep = ctx.enter_context(tc.tile_pool(name="keep", bufs=1))
+        shared = ctx.enter_context(tc.tile_pool(name="shared", bufs=1))
         psum = ctx.enter_context(tc.psum_pool(name="psum", bufs=1))
 
         offsets = keep.tile([P, S // 16], U16, name="offsets")
@@ -39,16 +41,16 @@ def tile_picked_modgate_mlpsilu_p_kernel(tc, x_words, x_scales, gate, w1, w2, of
         nc.sync.dma_start(out=w1_raw[0][:, 0:2, :], in_=w1_rows[0, :, 0:2, :])
         nc.sync.dma_start(offsets[:], offs)
 
-        xs_win = keep.tile([P, PASSES, T], U8, name="xs_win", align_bytes=64)
+        xs_win = shared.tile([P, PASSES, T], U8, name="xs_win", offset=0, align_bytes=64)
         nc.vector.memset(xs_win[:].bitcast(I32), 0)
         nc.sync.dma_start(out=xs_win[4:P:8, :, :].bitcast(I32), in_=x_scales.rearrange("z r c -> r z c").bitcast(I32))
         nc.sync.dma_start(out=w1_raw[0][:, 2:4, :], in_=w1_rows[0, :, 2:4, :])
-        nc.sync.dma_start(out=w1_raw[1][:, 0:2, :], in_=w1_rows[1, :, 0:2, :])
 
         g_win = keep.tile([P, T], F32, name="g_win", align_bytes=64)
-        nc.vector.memset(g_win[:].bitcast(I32), 0)
+        zero = keep.tile([P, CH], F32, name="zero")
+        nc.gpsimd.memset(zero[:], 0.0)
+        nc.vector.tensor_copy(out=g_win[:], in_=zero[:, 0:1].to_broadcast([P, T]))
         nc.sync.dma_start(out=g_win[GROW : GROW + 1, :], in_=gate[0:1, :])
-        nc.sync.dma_start(out=w1_raw[1][:, 2:4, :], in_=w1_rows[1, :, 2:4, :])
 
         ident = keep.tile([P, P], F32, name="ident")
         nc.vector.memset(ident[:], 0.0)
@@ -56,42 +58,32 @@ def tile_picked_modgate_mlpsilu_p_kernel(tc, x_words, x_scales, gate, w1, w2, of
 
         x_win = [keep.tile([P, T], I32, name="x_win0", align_bytes=64)]
         nc.sync.dma_start(out=x_win[0][:], in_=x_words[0].rearrange("p n t -> p (n t)").bitcast(I32))
+        nc.sync.dma_start(out=w1_raw[1][:, 0:2, :], in_=w1_rows[1, :, 0:2, :])
+        nc.sync.dma_start(out=w1_raw[1][:, 2:4, :], in_=w1_rows[1, :, 2:4, :])
 
         out_win = keep.tile([P, T], F32, name="out_win")
-        zero = keep.tile([P, CH], F32, name="zero")
-        nc.gpsimd.memset(zero[:], 0.0)
         nc.scalar.activation(out=out_win[:], in_=zero[:, 0:1].to_broadcast([P, T]), func=SILU)
 
         xs_apart = keep.tile([P, PASSES * S], U8, name="xs_apart", align_bytes=64)
         for z in range(PASSES):
             nc.vector.tensor_copy(xs_apart[:, z * S : (z + 1) * S], xs_win[:, z, :].indirect(offsets[:]))
-        xs = keep.tile([P, PASSES * S], U8, name="xs", tag="xs_win", align_bytes=64)
+        xs = shared.tile([P, PASSES * S], U8, name="xs", offset=0, align_bytes=64)
         for q in (0, 2, 1, 3):
             nc.sync.dma_start(out=xs[32 * q : 32 * q + 4, :].bitcast(I32), in_=xs_apart[32 * q + 4 : 32 * q + 32 : 8, :].bitcast(I32))
-        x_win.append(keep.tile([P, T], I32, name="x_win1", align_bytes=64))
+        x_win.append(shared.tile([P, T], I32, name="x_win1", offset=PASSES * S, align_bytes=64))
         nc.sync.dma_start(out=x_win[1][:], in_=x_words[1].rearrange("p n t -> p (n t)").bitcast(I32))
-        g_row = keep.tile([P, S], F32, name="g_row", align_bytes=64)
-        nc.vector.tensor_copy(g_row[:], g_win[:].indirect(offsets[:]))
-
-        turned = psum.tile([P, S // P, P], F32, name="turned")
-        for c in range(S // P):
-            nc.tensor.transpose(turned[:, c, :], g_row[:, c * P : (c + 1) * P], ident[:])
-        g_col = keep.tile([P, S // P], F32, name="g_col")
-        nc.vector.tensor_copy(out=g_col[:], in_=turned[:, :, GROW])
-        spread = psum.tile([P, S // P, P], F32, name="spread")
-        for c in range(S // P):
-            nc.tensor.transpose(spread[:, c, :], g_col[:, c : c + 1].to_broadcast([P, P]), ident[:])
 
         w1_bf = [[], []]
         w1_codes = [[], []]
         w1_scales = [[], []]
 
-        def cast_w1(z, parts):
+        def cast_w1(z, tag):
             src = w1_raw[z][:].rearrange("p j (m t) -> p m j t", t=PACK)
-            per = PACK // parts
-            for e in range(parts):
-                grouped = keep.tile([P, per, P, PACK], BF16, name="w1_bf%d%d" % (z, e), align_bytes=64)
-                nc.scalar.copy(out=grouped[:].rearrange("p t m j -> p m j t"), in_=src[:, :, :, per * e : per * (e + 1)])
+            per = PACK // 2
+            for e, copy in enumerate((nc.vector.tensor_copy, nc.scalar.copy)):
+                name = "w1_bf%d%d" % (z, e)
+                grouped = keep.tile([P, per, P, PACK], BF16, name=name, tag=tag if e else name, align_bytes=64)
+                copy(out=grouped[:].rearrange("p t m j -> p m j t"), in_=src[:, :, :, per * e : per * (e + 1)])
                 w1_bf[z].append(grouped)
 
         def quantise_w1(z, e, tag):
@@ -103,9 +95,22 @@ def tile_picked_modgate_mlpsilu_p_kernel(tc, x_words, x_scales, gate, w1, w2, of
                 w1_codes[z].append(codes[:, t * P : (t + 1) * P])
                 w1_scales[z].append(scales[:, t * P : (t + 1) * P])
 
-        cast_w1(0, 1)
-        cast_w1(1, 2)
-        quantise_w1(0, 0, "g_win")
+        g_row = keep.tile([P, S], F32, name="g_row", align_bytes=64)
+        nc.scalar.activation(out=g_row[:], in_=g_win[:].indirect(offsets[:]), func=COPY)
+
+        cast_w1(0, "g_win")
+        turned = psum.tile([P, S // P, P], F32, name="turned")
+        for c in range(S // P):
+            nc.tensor.transpose(turned[:, c, :], g_row[:, c * P : (c + 1) * P], ident[:])
+        g_col = keep.tile([P, S // P], F32, name="g_col", align_bytes=64)
+        nc.scalar.copy(out=g_col[:], in_=turned[:, :, GROW])
+        spread = psum.tile([P, S // P, P], F32, name="spread")
+        for c in range(S // P):
+            nc.tensor.transpose(spread[:, c, :], g_col[:, c : c + 1].to_broadcast([P, P]), ident[:])
+
+        quantise_w1(0, 0, "w1_codes00")
+        quantise_w1(0, 1, "w1_codes01")
+        cast_w1(1, "g_col")
 
         w2_raw = keep.tile([P, PACK, N], F32, name="w2_raw", tag="xs_apart", align_bytes=64)
         nc.sync.dma_start(out=w2_raw[:], in_=w2.rearrange("(p j) n -> p j n", j=PACK))
@@ -114,15 +119,19 @@ def tile_picked_modgate_mlpsilu_p_kernel(tc, x_words, x_scales, gate, w1, w2, of
         nc.scalar.copy(out=g[:], in_=spread[:].rearrange("p c n -> p (c n)"))
         xg = [[], []]
 
-        def gather_words(z, u, tag):
-            picked = keep.tile([P, HALF], U32, name="xg%d%d" % (z, u), tag=tag, align_bytes=64)
-            nc.vector.tensor_copy(picked[:], x_win[z][:].bitcast(U32).indirect(offsets[:, 16 * u : 16 * u + 16]))
-            xg[z].append(picked)
+        def gather_words(z, lo, hi, tag, piece=HALF):
+            picked = keep.tile([P, hi - lo], U32, name="xg%d_%d" % (z, lo), tag=tag, align_bytes=64)
+            for a in range(lo, hi, piece):
+                nc.vector.tensor_copy(
+                    picked[:, a - lo : a - lo + piece], x_win[z][:].bitcast(U32).indirect(offsets[:, a // 16 : (a + piece) // 16])
+                )
+            for c in range((hi - lo) // CH):
+                xg[z].append(picked[:, c * CH : (c + 1) * CH])
 
         accs = [psum.tile([P, PACK, CH], F32, name="acc%d" % c) for c in range(S // CH)]
 
         def first_layer(c, z):
-            words = xg[z][c // 2][:, (c % 2) * CH : (c % 2 + 1) * CH]
+            words = xg[z][c]
             for t in range(PACK):
                 nc.tensor.matmul_mx(
                     out=accs[c][:, t, :],
@@ -134,20 +143,20 @@ def tile_picked_modgate_mlpsilu_p_kernel(tc, x_words, x_scales, gate, w1, w2, of
                     stop=(z == PASSES - 1 and t == PACK - 1),
                 )
 
-        for u in range(2):
-            gather_words(0, u, "g_row" if u == 0 else "xg01")
+        gather_words(0, 0, HALF, "xg00")
+        gather_words(0, HALF, S, "xg01")
         quantise_w1(1, 0, "w1_codes10")
         quantise_w1(1, 1, "x_win0")
         for c in range(S // CH):
             first_layer(c, 0)
-        for u in range(2):
-            gather_words(1, u, "w1_bf1%d" % u)
+        gather_words(1, 0, HALF, "w1_bf10", CH)
+        gather_words(1, HALF, S, "g_col")
 
         w2_bf = keep.tile([P, N, PACK], BF16, name="w2_bf", align_bytes=64)
         nc.scalar.copy(
             out=w2_bf[:].rearrange("p (c i) j -> p c j i", i=4), in_=w2_raw[:].rearrange("p j (c i) -> p c j i", i=4)
         )
-        w2_codes = keep.tile([P, N], U32, name="w2_codes", tag="x_win1", align_bytes=64)
+        w2_codes = shared.tile([P, N], U32, name="w2_codes", offset=PASSES * S, align_bytes=64)
         w2_scales = keep.tile([P, N], U8, name="w2_scales", align_bytes=64)
         nc.vector.quantize_mx(out=w2_codes[:].bitcast(FP8X4), scales=w2_scales[:], in_=w2_bf[:].rearrange("p n j -> p (n j)"))
 

@@ -160,27 +160,26 @@ def tile_picked_modgate_mlpsilu_p_kernel(tc, x_words, x_scales, gate, w1, w2, of
         w2_scales = keep.tile([P, N], U8, name="w2_scales", align_bytes=64)
         nc.vector.quantize_mx(out=w2_codes[:].bitcast(FP8X4), scales=w2_scales[:], in_=w2_bf[:].rearrange("p n j -> p (n j)"))
 
-        h_all = keep.tile([P, S], U32, name="h_all", align_bytes=64)
-        y_first = psum.tile([P, FIRST], F32, name="y_first", tag="turned")
-        y_second = psum.tile([P, FIRST], F32, name="y_second", tag="spread")
-        y_mid = psum.tile([P, HALF], F32, name="y_mid")
-        y_last = psum.tile([P, CH], F32, name="y_last")
+        h_codes = keep.tile([P, S], U32, name="h_codes", align_bytes=64)
+        h_scales = keep.tile([P, S], U8, name="h_scales", align_bytes=64)
         for c in range(S // CH):
             first_layer(c, 1)
 
-        def hidden(lo, hi, y_ps):
+        def hidden(lo, hi):
             acc = accs[lo // CH][:, :, lo % CH : lo % CH + hi - lo]
             h_bf = keep.tile([P, hi - lo, PACK], BF16, name="h_bf%d" % lo, align_bytes=64)
             nc.scalar.activation(out=h_bf[:], in_=acc.rearrange("p t n -> p n t"), func=SILU)
-            h_codes = h_all[:, lo:hi]
-            h_scales = keep.tile([P, hi - lo], U8, name="h_scales%d" % lo, align_bytes=64)
-            nc.vector.quantize_mx(out=h_codes.bitcast(FP8X4), scales=h_scales[:], in_=h_bf[:].rearrange("p n t -> p (n t)"))
+            nc.vector.quantize_mx(
+                out=h_codes[:, lo:hi].bitcast(FP8X4), scales=h_scales[:, lo:hi], in_=h_bf[:].rearrange("p n t -> p (n t)")
+            )
+
+        def second_layer(lo, hi, y_ps):
             nc.tensor.matmul_mx(
                 out=y_ps,
                 lhsT=w2_codes[:].bitcast(FP8X4),
                 lhsT_scale=w2_scales[:],
-                rhs=h_codes.bitcast(FP8X4),
-                rhs_scale=h_scales[:],
+                rhs=h_codes[:, lo:hi].bitcast(FP8X4),
+                rhs_scale=h_scales[:, lo:hi],
                 start=True,
                 stop=True,
             )
@@ -193,20 +192,31 @@ def tile_picked_modgate_mlpsilu_p_kernel(tc, x_words, x_scales, gate, w1, w2, of
         def place(lo, hi, yg, zeros):
             nc.vector.tensor_tensor(out_win[:].indirect(offsets[:, lo // 16 : hi // 16]), yg[:], zeros, ADD)
 
-        hidden(0, FIRST, y_first[:])
-        hidden(FIRST, CH, y_second[:])
-        yg_first = weigh(0, FIRST, y_first[:])
-        hidden(CH, HALF, y_mid[:, :CH])
-        yg_second = weigh(FIRST, CH, y_second[:])
-        place(0, FIRST, yg_first, zero[:, :FIRST])
-        hidden(HALF, HALF + CH, y_mid[:, CH:])
-        hidden(HALF + CH, S - FIRST, y_last[:, :FIRST])
-        hidden(S - FIRST, S, y_last[:, FIRST:])
-        zeros_second = keep.tile([P, FIRST], F32, name="zeros_second", tag="h_bf%d" % HALF, align_bytes=64)
-        nc.scalar.copy(out=zeros_second[:], in_=zero[:, 0:1].to_broadcast([P, FIRST]))
-        place(FIRST, CH, yg_second, zeros_second[:])
-        y_sb = keep.tile([P, S - CH], F32, name="y_sb")
-        nc.scalar.copy(out=y_sb[:, :HALF], in_=y_mid[:])
-        nc.scalar.copy(out=y_sb[:, HALF:], in_=y_last[:])
-        nc.vector.tensor_tensor(out_win[:].indirect(offsets[:, CH // 16 : S // 16]), y_sb[:], g[:, CH:S], MULT)
+        y_first = psum.tile([P, FIRST], F32, name="y_first", tag="turned")
+        y_second = psum.tile([P, CH], F32, name="y_second", tag="spread")
+        y_mid = psum.tile([P, 192], F32, name="y_mid")
+        y_last = psum.tile([P, CH], F32, name="y_last")
+        hidden(0, 64)
+        second_layer(0, 64, y_first[:])
+        hidden(64, 128)
+        yg_first = weigh(0, 64, y_first[:])
+        hidden(128, 192)
+        second_layer(64, 192, y_second[:])
+        hidden(192, 256)
+        second_layer(192, 256, y_mid[:, :64])
+        place(0, 64, yg_first, zero[:, :FIRST])
+        hidden(256, 384)
+        second_layer(256, 384, y_mid[:, 64:])
+        yg_second = weigh(64, 192, y_second[:])
+        hidden(384, 448)
+        second_layer(384, 448, y_last[:, :64])
+        hidden(448, 512)
+        second_layer(448, 512, y_last[:, 64:])
+        zeros_second = keep.tile([P, CH], F32, name="zeros_second", tag="h_bf192", align_bytes=64)
+        nc.scalar.copy(out=zeros_second[:], in_=zero[:, 0:1].to_broadcast([P, CH]))
+        place(64, 192, yg_second, zeros_second[:])
+        y_sb = keep.tile([P, 320], F32, name="y_sb")
+        nc.scalar.copy(out=y_sb[:, :192], in_=y_mid[:])
+        nc.scalar.copy(out=y_sb[:, 192:], in_=y_last[:])
+        nc.vector.tensor_tensor(out_win[:].indirect(offsets[:, 192 // 16 : S // 16]), y_sb[:], g[:, 192:S], MULT)
         nc.sync.dma_start(out=out, in_=out_win[:])

@@ -41,9 +41,9 @@ def tile_picked_modgate_mlpsilu_p_kernel(tc, x_words, x_scales, gate, w1, w2, of
         nc.sync.dma_start(out=w1_raw[0][:, 0:2, :], in_=w1_rows[0, :, 0:2, :])
         nc.sync.dma_start(offsets[:], offs)
 
-        xs_win = shared.tile([P, PASSES, T], U8, name="xs_win", offset=0, align_bytes=64)
+        xs_win = shared.tile([P, T], U8, name="xs_win", offset=0, align_bytes=64)
         nc.vector.memset(xs_win[:].bitcast(I32), 0)
-        nc.sync.dma_start(out=xs_win[4:P:8, :, :].bitcast(I32), in_=x_scales.rearrange("z r c -> r z c").bitcast(I32))
+        nc.sync.dma_start(out=xs_win[0:P:4, :].bitcast(I32), in_=x_scales.rearrange("z r c -> (z r) c").bitcast(I32))
         nc.sync.dma_start(out=w1_raw[0][:, 2:4, :], in_=w1_rows[0, :, 2:4, :])
 
         g_win = keep.tile([P, T], F32, name="g_win", align_bytes=64)
@@ -64,12 +64,16 @@ def tile_picked_modgate_mlpsilu_p_kernel(tc, x_words, x_scales, gate, w1, w2, of
         out_win = keep.tile([P, T], F32, name="out_win")
         nc.scalar.activation(out=out_win[:], in_=zero[:, 0:1].to_broadcast([P, T]), func=SILU)
 
+        xs_picked = keep.tile([P, S], U8, name="xs_picked", align_bytes=64)
+        nc.vector.tensor_copy(xs_picked[:], xs_win[:].indirect(offsets[:]))
         xs_apart = keep.tile([P, PASSES * S], U8, name="xs_apart", align_bytes=64)
         for z in range(PASSES):
-            nc.vector.tensor_copy(xs_apart[:, z * S : (z + 1) * S], xs_win[:, z, :].indirect(offsets[:]))
+            nc.vector.tensor_copy(
+                out=xs_apart[0:64, z * S : (z + 1) * S].bitcast(I32), in_=xs_picked[64 * z : 64 * z + 64, :].bitcast(I32)
+            )
         xs = shared.tile([P, PASSES * S], U8, name="xs", offset=0, align_bytes=64)
         for q in (0, 2, 1, 3):
-            nc.sync.dma_start(out=xs[32 * q : 32 * q + 4, :].bitcast(I32), in_=xs_apart[32 * q + 4 : 32 * q + 32 : 8, :].bitcast(I32))
+            nc.sync.dma_start(out=xs[32 * q : 32 * q + 4, :].bitcast(I32), in_=xs_apart[16 * q : 16 * q + 16 : 4, :].bitcast(I32))
         x_win.append(shared.tile([P, T], I32, name="x_win1", offset=PASSES * S, align_bytes=64))
         nc.sync.dma_start(out=x_win[1][:], in_=x_words[1].rearrange("p n t -> p (n t)").bitcast(I32))
 

@@ -46,7 +46,7 @@ def tile_picked_modgate_mlpsilu_p_kernel(tc, x_words, x_scales, gate, w1, w2, of
         nc.sync.dma_start(out=xs_win[0:P:4, :].bitcast(I32), in_=x_scales.rearrange("z r c -> (z r) c").bitcast(I32))
         nc.sync.dma_start(out=w1_raw[0][:, 2:4, :], in_=w1_rows[0, :, 2:4, :])
 
-        g_win = keep.tile([P, T], F32, name="g_win", align_bytes=64)
+        g_win = shared.tile([P, T], F32, name="g_win", offset=T, align_bytes=64)
         zero = keep.tile([P, CH], F32, name="zero")
         nc.gpsimd.memset(zero[:], 0.0)
         nc.vector.tensor_copy(out=g_win[:], in_=zero[:, 0:1].to_broadcast([P, T]))
@@ -59,10 +59,10 @@ def tile_picked_modgate_mlpsilu_p_kernel(tc, x_words, x_scales, gate, w1, w2, of
         x_win = [keep.tile([P, T], I32, name="x_win0", align_bytes=64)]
         nc.sync.dma_start(out=x_win[0][:], in_=x_words[0].rearrange("p n t -> p (n t)").bitcast(I32))
         nc.sync.dma_start(out=w1_raw[1][:, 0:2, :], in_=w1_rows[1, :, 0:2, :])
-        nc.sync.dma_start(out=w1_raw[1][:, 2:4, :], in_=w1_rows[1, :, 2:4, :])
 
         out_win = keep.tile([P, T], F32, name="out_win")
-        nc.scalar.activation(out=out_win[:], in_=zero[:, 0:1].to_broadcast([P, T]), func=SILU)
+        nc.gpsimd.memset(w1_raw[1][:, 2, 0:8], 0.0)
+        nc.scalar.activation(out=out_win[:], in_=w1_raw[1][:, 2, 0:1].to_broadcast([P, T]), func=SILU)
 
         xs_picked = keep.tile([P, S], U8, name="xs_picked", align_bytes=64)
         nc.vector.tensor_copy(xs_picked[:], xs_win[:].indirect(offsets[:]))
@@ -74,7 +74,10 @@ def tile_picked_modgate_mlpsilu_p_kernel(tc, x_words, x_scales, gate, w1, w2, of
         xs = shared.tile([P, PASSES * S], U8, name="xs", offset=0, align_bytes=64)
         for q in (0, 2, 1, 3):
             nc.sync.dma_start(out=xs[32 * q : 32 * q + 4, :].bitcast(I32), in_=xs_apart[16 * q : 16 * q + 16 : 4, :].bitcast(I32))
-        x_win.append(shared.tile([P, T], I32, name="x_win1", offset=PASSES * S, align_bytes=64))
+        nc.sync.dma_start(out=w1_raw[1][:, 2:4, :], in_=w1_rows[1, :, 2:4, :])
+        g_row = keep.tile([P, S], F32, name="g_row", align_bytes=64)
+        nc.scalar.activation(out=g_row[:], in_=g_win[:].indirect(offsets[:]), func=COPY)
+        x_win.append(shared.tile([P, T], I32, name="x_win1", offset=3 * T, align_bytes=64))
         nc.sync.dma_start(out=x_win[1][:], in_=x_words[1].rearrange("p n t -> p (n t)").bitcast(I32))
 
         w1_bf = [[], []]
@@ -86,7 +89,10 @@ def tile_picked_modgate_mlpsilu_p_kernel(tc, x_words, x_scales, gate, w1, w2, of
             per = PACK // 2
             for e, copy in enumerate((nc.vector.tensor_copy, nc.scalar.copy)):
                 name = "w1_bf%d%d" % (z, e)
-                grouped = keep.tile([P, per, P, PACK], BF16, name=name, tag=tag if e else name, align_bytes=64)
+                if e and not z:
+                    grouped = shared.tile([P, per, P, PACK], BF16, name=name, offset=T, align_bytes=64)
+                else:
+                    grouped = keep.tile([P, per, P, PACK], BF16, name=name, tag=tag if e else name, align_bytes=64)
                 copy(out=grouped[:].rearrange("p t m j -> p m j t"), in_=src[:, :, :, per * e : per * (e + 1)])
                 w1_bf[z].append(grouped)
 
@@ -99,8 +105,6 @@ def tile_picked_modgate_mlpsilu_p_kernel(tc, x_words, x_scales, gate, w1, w2, of
                 w1_codes[z].append(codes[:, t * P : (t + 1) * P])
                 w1_scales[z].append(scales[:, t * P : (t + 1) * P])
 
-        g_row = keep.tile([P, S], F32, name="g_row", align_bytes=64)
-        nc.scalar.activation(out=g_row[:], in_=g_win[:].indirect(offsets[:]), func=COPY)
 
         cast_w1(0, "g_win")
         turned = psum.tile([P, S // P, P], F32, name="turned")
@@ -160,7 +164,7 @@ def tile_picked_modgate_mlpsilu_p_kernel(tc, x_words, x_scales, gate, w1, w2, of
         nc.scalar.copy(
             out=w2_bf[:].rearrange("p (c i) j -> p c j i", i=4), in_=w2_raw[:].rearrange("p j (c i) -> p c j i", i=4)
         )
-        w2_codes = shared.tile([P, N], U32, name="w2_codes", offset=PASSES * S, align_bytes=64)
+        w2_codes = shared.tile([P, N], U32, name="w2_codes", offset=3 * T, align_bytes=64)
         w2_scales = keep.tile([P, N], U8, name="w2_scales", align_bytes=64)
         nc.vector.quantize_mx(out=w2_codes[:].bitcast(FP8X4), scales=w2_scales[:], in_=w2_bf[:].rearrange("p n j -> p (n j)"))
 

@@ -58,11 +58,11 @@ def tile_picked_modgate_mlpsilu_p_kernel(tc, x_words, x_scales, gate, w1, w2, of
 
         x_win = [keep.tile([P, T], I32, name="x_win0", align_bytes=64)]
         nc.sync.dma_start(out=x_win[0][:], in_=x_words[0].rearrange("p n t -> p (n t)").bitcast(I32))
-        nc.sync.dma_start(out=w1_raw[1][:, 0:2, :], in_=w1_rows[1, :, 0:2, :])
+        nc.sync.dma_start(out=w1_raw[1][:, 0:3, :], in_=w1_rows[1, :, 0:3, :])
 
         out_win = keep.tile([P, T], F32, name="out_win")
-        nc.gpsimd.memset(w1_raw[1][:, 2, 0:8], 0.0)
-        nc.scalar.activation(out=out_win[:], in_=w1_raw[1][:, 2, 0:1].to_broadcast([P, T]), func=SILU)
+        nc.gpsimd.memset(w1_raw[1][:, 3, 0:8], 0.0)
+        nc.scalar.activation(out=out_win[:], in_=w1_raw[1][:, 3, 0:1].to_broadcast([P, T]), func=SILU)
 
         xs_picked = keep.tile([P, S], U8, name="xs_picked", align_bytes=64)
         nc.vector.tensor_copy(xs_picked[:], xs_win[:].indirect(offsets[:]))
@@ -74,7 +74,7 @@ def tile_picked_modgate_mlpsilu_p_kernel(tc, x_words, x_scales, gate, w1, w2, of
         xs = shared.tile([P, PASSES * S], U8, name="xs", offset=0, align_bytes=64)
         for q in (0, 2, 1, 3):
             nc.sync.dma_start(out=xs[32 * q : 32 * q + 4, :].bitcast(I32), in_=xs_apart[16 * q : 16 * q + 16 : 4, :].bitcast(I32))
-        nc.sync.dma_start(out=w1_raw[1][:, 2:4, :], in_=w1_rows[1, :, 2:4, :])
+        nc.sync.dma_start(out=w1_raw[1][:, 3:4, :], in_=w1_rows[1, :, 3:4, :])
         g_row = keep.tile([P, S], F32, name="g_row", align_bytes=64)
         nc.scalar.activation(out=g_row[:], in_=g_win[:].indirect(offsets[:]), func=COPY)
         x_win.append(shared.tile([P, T], I32, name="x_win1", offset=3 * T, align_bytes=64))

@@ -47,7 +47,7 @@ def tile_picked_modgate_mlpsilu_p_kernel(tc, x_words, x_scales, gate, w1, w2, of
         nc.sync.dma_start(out=w1_raw[0][:, 2:4, :], in_=w1_rows[0, :, 2:4, :])
 
         g_win = shared.tile([P, T], F32, name="g_win", offset=T, align_bytes=64)
-        zero = keep.tile([P, CH], F32, name="zero")
+        zero = keep.tile([P, FIRST], F32, name="zero")
         nc.gpsimd.memset(zero[:], 0.0)
         nc.vector.tensor_copy(out=g_win[:], in_=zero[:, 0:1].to_broadcast([P, T]))
         nc.sync.dma_start(out=g_win[GROW : GROW + 1, :], in_=gate[0:1, :])
@@ -61,7 +61,7 @@ def tile_picked_modgate_mlpsilu_p_kernel(tc, x_words, x_scales, gate, w1, w2, of
         nc.sync.dma_start(out=w1_raw[1][:, 0:3, :], in_=w1_rows[1, :, 0:3, :])
 
         out_win = keep.tile([P, T], F32, name="out_win")
-        nc.gpsimd.memset(w1_raw[1][:, 3, 0:8], 0.0)
+        nc.gpsimd.memset(w1_raw[1][:, 3, 0:1], 0.0)
         nc.scalar.activation(out=out_win[:], in_=w1_raw[1][:, 3, 0:1].to_broadcast([P, T]), func=SILU)
 
         xs_picked = keep.tile([P, S], U8, name="xs_picked", align_bytes=64)

from contextlib import ExitStack

import concourse.mybir as mybir
from concourse.masks import make_identity

K, T, S, H, N = 1024, 2048, 512, 512, 128
FLOPS = 2 * S * (K * H + H * N)
BYTES = K * T + (K // 32) * T + 4 * T + 4 * K * H + 4 * H * N + 2 * 128 * (S // 16) + 4 * N * T

F32 = mybir.dt.float32
BF16 = mybir.dt.bfloat16
I32 = mybir.dt.int32
U32 = mybir.dt.uint32
U16 = mybir.dt.uint16
U8 = mybir.dt.uint8
FP8X4 = mybir.dt.float8_e4m3fn_x4
SILU = mybir.ActivationFunctionType.Silu
COPY = mybir.ActivationFunctionType.Copy
MULT = mybir.AluOpType.mult
ADD = mybir.AluOpType.add

P = 128
PACK = 4
PASSES = K // (P * PACK)
CH = 128
HALF = 256
GROW = 8
FIRST = 64


def tile_picked_modgate_mlpsilu_p_kernel(tc, x_words, x_scales, gate, w1, w2, offs, out):
    nc = tc.nc
    with ExitStack() as ctx:
        keep = ctx.enter_context(tc.tile_pool(name="keep", bufs=1))
        shared = ctx.enter_context(tc.tile_pool(name="shared", bufs=1))
        psum = ctx.enter_context(tc.psum_pool(name="psum", bufs=1))

        offsets = keep.tile([P, S // 16], U16, name="offsets")
        w1_raw = [keep.tile([P, PACK, H], F32, name="w1_raw%d" % z, align_bytes=64) for z in range(PASSES)]
        w1_rows = w1.rearrange("(z p j) c -> z p j c", z=PASSES, j=PACK)
        nc.sync.dma_start(out=w1_raw[0][:, 0:2, :], in_=w1_rows[0, :, 0:2, :])
        nc.sync.dma_start(offsets[:], offs)

        xs_win = shared.tile([P, T], U8, name="xs_win", offset=0, align_bytes=64)
        nc.vector.memset(xs_win[:].bitcast(I32), 0)
        nc.sync.dma_start(out=xs_win[0:P:4, :].bitcast(I32), in_=x_scales.rearrange("z r c -> (z r) c").bitcast(I32))
        nc.sync.dma_start(out=w1_raw[0][:, 2:4, :], in_=w1_rows[0, :, 2:4, :])

        g_win = shared.tile([P, T], F32, name="g_win", offset=T, align_bytes=64)
        zero = keep.tile([P, FIRST], F32, name="zero")
        nc.gpsimd.memset(zero[:], 0.0)
        nc.vector.tensor_copy(out=g_win[:], in_=zero[:, 0:1].to_broadcast([P, T]))
        nc.sync.dma_start(out=g_win[GROW : GROW + 1, :], in_=gate[0:1, :])

        ident = keep.tile([P, P], F32, name="ident")
        nc.vector.memset(ident[:], 0.0)
        make_identity(nc, ident[:], nomemset=True)

        x_win = [keep.tile([P, T], I32, name="x_win0", align_bytes=64)]
        nc.sync.dma_start(out=x_win[0][:], in_=x_words[0].rearrange("p n t -> p (n t)").bitcast(I32))
        nc.sync.dma_start(out=w1_raw[1][:, 0:3, :], in_=w1_rows[1, :, 0:3, :])

        out_win = keep.tile([P, T], F32, name="out_win")
        nc.gpsimd.memset(w1_raw[1][:, 3, 0:1], 0.0)
        nc.scalar.activation(out=out_win[:], in_=w1_raw[1][:, 3, 0:1].to_broadcast([P, T]), func=SILU)

        xs_picked = keep.tile([P, S], U8, name="xs_picked", align_bytes=64)
        nc.vector.tensor_copy(xs_picked[:], xs_win[:].indirect(offsets[:]))
        xs_apart = keep.tile([P, PASSES * S], U8, name="xs_apart", align_bytes=64)
        for z in range(PASSES):
            nc.vector.tensor_copy(
                out=xs_apart[0:64, z * S : (z + 1) * S].bitcast(I32), in_=xs_picked[64 * z : 64 * z + 64, :].bitcast(I32)
            )
        xs = shared.tile([P, PASSES * S], U8, name="xs", offset=0, align_bytes=64)
        for q in (0, 2, 1, 3):
            nc.sync.dma_start(out=xs[32 * q : 32 * q + 4, :].bitcast(I32), in_=xs_apart[16 * q : 16 * q + 16 : 4, :].bitcast(I32))
        nc.sync.dma_start(out=w1_raw[1][:, 3:4, :], in_=w1_rows[1, :, 3:4, :])
        g_row = keep.tile([P, S], F32, name="g_row", align_bytes=64)
        nc.scalar.activation(out=g_row[:], in_=g_win[:].indirect(offsets[:]), func=COPY)
        x_win.append(shared.tile([P, T], I32, name="x_win1", offset=3 * T, align_bytes=64))
        nc.sync.dma_start(out=x_win[1][:], in_=x_words[1].rearrange("p n t -> p (n t)").bitcast(I32))

        w1_bf = [[], []]
        w1_codes = [[], []]
        w1_scales = [[], []]

        def cast_w1(z, tag):
            src = w1_raw[z][:].rearrange("p j (m t) -> p m j t", t=PACK)
            per = PACK // 2
            for e, copy in enumerate((nc.vector.tensor_copy, nc.scalar.copy)):
                name = "w1_bf%d%d" % (z, e)
                if e and not z:
                    grouped = shared.tile([P, per, P, PACK], BF16, name=name, offset=T, align_bytes=64)
                else:
                    grouped = keep.tile([P, per, P, PACK], BF16, name=name, tag=tag if e else name, align_bytes=64)
                copy(out=grouped[:].rearrange("p t m j -> p m j t"), in_=src[:, :, :, per * e : per * (e + 1)])
                w1_bf[z].append(grouped)

        def quantise_w1(z, e, tag):
            per = PACK // len(w1_bf[z])
            codes = keep.tile([P, per * P], U32, name="w1_codes%d%d" % (z, e), tag=tag, align_bytes=64)
            scales = keep.tile([P, per * P], U8, name="w1_scales%d%d" % (z, e), align_bytes=64)
            nc.vector.quantize_mx(out=codes[:].bitcast(FP8X4), scales=scales[:], in_=w1_bf[z][e][:].rearrange("p t m j -> p (t m j)"))
            for t in range(per):
                w1_codes[z].append(codes[:, t * P : (t + 1) * P])
                w1_scales[z].append(scales[:, t * P : (t + 1) * P])


        cast_w1(0, "g_win")
        turned = psum.tile([P, S // P, P], F32, name="turned")
        for c in range(S // P):
            nc.tensor.transpose(turned[:, c, :], g_row[:, c * P : (c + 1) * P], ident[:])
        g_col = keep.tile([P, S // P], F32, name="g_col", align_bytes=64)
        nc.scalar.copy(out=g_col[:], in_=turned[:, :, GROW])
        spread = psum.tile([P, S // P, P], F32, name="spread")
        for c in range(S // P):
            nc.tensor.transpose(spread[:, c, :], g_col[:, c : c + 1].to_broadcast([P, P]), ident[:])

        quantise_w1(0, 0, "w1_codes00")
        quantise_w1(0, 1, "w1_codes01")
        cast_w1(1, "g_col")

        w2_raw = keep.tile([P, PACK, N], F32, name="w2_raw", tag="xs_apart", align_bytes=64)
        nc.sync.dma_start(out=w2_raw[:], in_=w2.rearrange("(p j) n -> p j n", j=PACK))

        g = keep.tile([P, S], F32, name="g", tag="w1_raw1", align_bytes=64)
        nc.scalar.copy(out=g[:], in_=spread[:].rearrange("p c n -> p (c n)"))
        xg = [[], []]

        def gather_words(z, lo, hi, tag, piece=HALF):
            picked = keep.tile([P, hi - lo], U32, name="xg%d_%d" % (z, lo), tag=tag, align_bytes=64)
            for a in range(lo, hi, piece):
                nc.vector.tensor_copy(
                    picked[:, a - lo : a - lo + piece], x_win[z][:].bitcast(U32).indirect(offsets[:, a // 16 : (a + piece) // 16])
                )
            for c in range((hi - lo) // CH):
                xg[z].append(picked[:, c * CH : (c + 1) * CH])

        accs = [psum.tile([P, PACK, CH], F32, name="acc%d" % c) for c in range(S // CH)]

        def first_layer(c, z):
            words = xg[z][c]
            for t in range(PACK):
                nc.tensor.matmul_mx(
                    out=accs[c][:, t, :],
                    lhsT=w1_codes[z][t].bitcast(FP8X4),
                    lhsT_scale=w1_scales[z][t],
                    rhs=words.bitcast(FP8X4),
                    rhs_scale=xs[:, z * S + c * CH : z * S + (c + 1) * CH],
                    start=(z == 0 and t == 0),
                    stop=(z == PASSES - 1 and t == PACK - 1),
                )

        gather_words(0, 0, HALF, "xg00")
        gather_words(0, HALF, S, "xg01")
        quantise_w1(1, 0, "w1_codes10")
        quantise_w1(1, 1, "x_win0")
        for c in range(S // CH):
            first_layer(c, 0)
        gather_words(1, 0, HALF, "w1_bf10", CH)
        gather_words(1, HALF, S, "g_col")

        w2_bf = keep.tile([P, N, PACK], BF16, name="w2_bf", align_bytes=64)
        nc.scalar.copy(
            out=w2_bf[:].rearrange("p (c i) j -> p c j i", i=4), in_=w2_raw[:].rearrange("p j (c i) -> p c j i", i=4)
        )
        w2_codes = shared.tile([P, N], U32, name="w2_codes", offset=3 * T, align_bytes=64)
        w2_scales = keep.tile([P, N], U8, name="w2_scales", align_bytes=64)
        nc.vector.quantize_mx(out=w2_codes[:].bitcast(FP8X4), scales=w2_scales[:], in_=w2_bf[:].rearrange("p n j -> p (n j)"))

        h_codes = keep.tile([P, S], U32, name="h_codes", align_bytes=64)
        h_scales = keep.tile([P, S], U8, name="h_scales", align_bytes=64)
        for c in range(S // CH):
            first_layer(c, 1)

        def hidden(lo, hi):
            acc = accs[lo // CH][:, :, lo % CH : lo % CH + hi - lo]
            h_bf = keep.tile([P, hi - lo, PACK], BF16, name="h_bf%d" % lo, align_bytes=64)
            nc.scalar.activation(out=h_bf[:], in_=acc.rearrange("p t n -> p n t"), func=SILU)
            nc.vector.quantize_mx(
                out=h_codes[:, lo:hi].bitcast(FP8X4), scales=h_scales[:, lo:hi], in_=h_bf[:].rearrange("p n t -> p (n t)")
            )

        def second_layer(lo, hi, y_ps):
            nc.tensor.matmul_mx(
                out=y_ps,
                lhsT=w2_codes[:].bitcast(FP8X4),
                lhsT_scale=w2_scales[:],
                rhs=h_codes[:, lo:hi].bitcast(FP8X4),
                rhs_scale=h_scales[:, lo:hi],
                start=True,
                stop=True,
            )

        def weigh(lo, hi, y_ps):
            yg = keep.tile([P, hi - lo], F32, name="yg%d" % lo)
            nc.vector.tensor_tensor(yg[:], y_ps, g[:, lo:hi], MULT)
            return yg

        def place(lo, hi, yg, zeros):
            nc.vector.tensor_tensor(out_win[:].indirect(offsets[:, lo // 16 : hi // 16]), yg[:], zeros, ADD)

        y_first = psum.tile([P, FIRST], F32, name="y_first", tag="turned")
        y_second = psum.tile([P, CH], F32, name="y_second", tag="spread")
        y_mid = psum.tile([P, 192], F32, name="y_mid")
        y_last = psum.tile([P, CH], F32, name="y_last")
        hidden(0, 64)
        second_layer(0, 64, y_first[:])
        hidden(64, 128)
        yg_first = weigh(0, 64, y_first[:])
        hidden(128, 192)
        second_layer(64, 192, y_second[:])
        hidden(192, 256)
        second_layer(192, 256, y_mid[:, :64])
        place(0, 64, yg_first, zero[:, :FIRST])
        hidden(256, 384)
        second_layer(256, 384, y_mid[:, 64:])
        yg_second = weigh(64, 192, y_second[:])
        hidden(384, 448)
        second_layer(384, 448, y_last[:, :64])
        hidden(448, 512)
        second_layer(448, 512, y_last[:, 64:])
        zeros_second = keep.tile([P, CH], F32, name="zeros_second", tag="h_bf192", align_bytes=64)
        nc.scalar.copy(out=zeros_second[:], in_=zero[:, 0:1].to_broadcast([P, CH]))
        place(64, 192, yg_second, zeros_second[:])
        y_sb = keep.tile([P, 320], F32, name="y_sb")
        nc.scalar.copy(out=y_sb[:, :192], in_=y_mid[:])
        nc.scalar.copy(out=y_sb[:, 192:], in_=y_last[:])
        nc.vector.tensor_tensor(out_win[:].indirect(offsets[:, 192 // 16 : S // 16]), y_sb[:], g[:, 192:S], MULT)
        nc.sync.dma_start(out=out, in_=out_win[:])
